import numpy as np, ml_dtypes
CORES = [3,11,19,27,35,43,51,59]
N = 8
import mx_ref
BF = ml_dtypes.bfloat16
def cols(t, e):
    v = np.concatenate([t.reshape(128, -1, 4), np.zeros((128, 1, 4), BF)], axis=1)
    return np.ascontiguousarray(v[:, e]).reshape(128, -1)
def cut(t, i, w=512):
    return t[:, w * i:w * i + w]
def f(rng, *shape):
    return mx_ref.flush((rng.standard_normal(shape, dtype=np.float32) * np.exp2(rng.integers(-2, 3, shape[:-1] + (1,)))).astype(BF))
def wide(rng, *shape, cols=0):
    v = rng.standard_normal(shape, dtype=np.float32) * np.exp2(rng.integers(-12, 13, shape)).astype(np.float32)
    if cols: v *= np.repeat(np.exp2(rng.integers(-cols, cols + 1, shape[:-2] + (1, shape[-1] // 4))) * (rng.random(shape[:-2] + (1, shape[-1] // 4)) > 0.0625), 4, axis=-1).astype(np.float32)
    return mx_ref.flush(v.astype(BF))
T, O, CH = 512, 2, 64
def order(x, u):
    score = mx_ref.matmul(mx_ref.quantize(u), mx_ref.quantize(x))[0] + np.float32(0.0)
    return np.lexsort((np.arange(T), -score))
def held(t):
    t = t.copy(); t[np.abs(t.astype(np.float32)) < 2.0 ** -30] = 0; return t
def first(v):
    t = np.zeros((N, 128, 512), BF); t[:, :, :4] = v; return t
def setup_inputs(rng):
    return {"x": held(f(rng, N, 128, 4 * T)), "u": first(held(f(rng, N, 128, 4))), "w": held(f(rng, N, 128, O * 512))}
def setup_inputs_ties(rng):
    d = setup_inputs(rng)
    for r in range(N):
        k = N - 1 if r % 2 else T // 8
        d["x"][r] = cols(d["x"][r], rng.permutation(T)[:k][rng.integers(0, k, T)])
    return d
def setup_inputs_falling(rng):
    d = setup_inputs(rng); d["x"] = np.stack([cols(d["x"][r], order(d["x"][r], d["u"][r])) for r in range(N)]); return d
def setup_inputs_near(rng):
    d = setup_inputs(rng); k = T // 8
    for r in range(N): d["x"][r] = cols(d["x"][r], rng.permutation(T)[:k][rng.permutation(T) % k])
    d["x"][:, :8] = held((f(rng, N, 8, 4 * T).astype(np.float32) * np.float32(2.0 ** -20)).astype(BF))
    return d
def setup_inputs_zeros(rng):
    d = setup_inputs(rng); d["u"][rng.permutation(N)[:N // 2]] = 0; return d
def setup_inputs_spread(rng):
    d = setup_inputs(rng); d["x"] = held(wide(rng, N, 128, 4 * T, cols=8)); d["u"] = first(held(wide(rng, N, 128, 4))); return d
def check_inputs(d):
    b = []
    for k in ("x", "u", "w"):
        a = np.abs(d[k].astype(np.float32))
        ok = ((a == 0) | ((a >= 2.0 ** -30) & (a <= 2.0 ** 30))).all()
        if k == "u" and not (a[:, :, 4:] == 0).all(): ok = False
        if not ok: b.append(k)
    return b
def reference(x, u, w):
    y = np.zeros((N, 128, N * O * CH), np.float32); ix = np.zeros((N, N, CH), np.float32)
    W = [[mx_ref.quantize(np.ascontiguousarray(cut(w[d], o))) for o in range(O)] for d in range(N)]
    for s in range(N):
        e = order(x[s], u[s])
        for d in range(N):
            run = e[d * CH:d * CH + CH]
            ix[d, s] = run
            t = mx_ref.quantize(cols(x[s], run))
            for o in range(O):
                k = (s * O + o) * CH
                y[d][:, k:k + CH] = mx_ref.matmul(W[d][o], t)
    return {"y": y, "ix": ix}

@@ -1,0 +1,346 @@
+from concourse.bass import DstId, RemoteDMATransfer
+from concourse.mybir import AluOpType, ActivationFunctionType
+
+N, TC, O, CH = 8, 512, 2, 64
+MX4 = "float8_e4m3fn_x4"
+SCRATCH = {
+    "UB": ("sbuf", [128, 16], "bfloat16"),
+    "UR": ("sbuf", [128, 512], "bfloat16"),
+    "UQ": ("sbuf", [128, 128], MX4), "US": ("sbuf", [128, 128], "uint8"),
+    "XB": ("sbuf", [128, 2048], "bfloat16"),
+    "XQ": ("sbuf", [128, 512], MX4), "XS": ("sbuf", [128, 512], "uint8"),
+    "WB": ("sbuf", [128, 1024], "bfloat16"),
+    "WQ": ("sbuf", [128, 256], MX4), "WS": ("sbuf", [128, 256], "uint8"),
+    "PI": ("sbuf", [128, 32], "int32"),
+    "UI": ("sbuf", [128, 32], "int32"), "UO": ("sbuf", [128, 32], "uint16"),
+    "GI": ("sbuf", [128, 8], "int32"), "GF": ("sbuf", [128, 8], "float32"),
+    "JF": ("sbuf", [128, 128], "float32"), "J": ("sbuf", [128, 128], "bfloat16"),
+    "ONE": ("sbuf", [128, 128], "bfloat16"), "MK": ("sbuf", [128, 128], "bfloat16"),
+    "C": ("sbuf", [128, 2560], "bfloat16"),
+    "EQ": ("sbuf", [128, 512], "bfloat16"),
+    "JK": ("sbuf", [128, 1560], "bfloat16"),
+    "CNT": ("sbuf", [128, 264], "float32"),
+    "XM": ("sbuf", [128, 8], "float32"), "OF": ("sbuf", [128, 8], "uint16"),
+    "SW": ("sbuf", [128, 1024], "bfloat16"), "TT": ("sbuf", [128, 1024], "bfloat16"),
+    "Z": ("sbuf", [128, 128], "bfloat16"), "HA": ("sbuf", [128, 64], "bfloat16"), "HB": ("sbuf", [128, 32], "bfloat16"),
+    "OT": ("sbuf", [128, 32], "uint16"),
+    "PL": ("sbuf", [128, 2048], "bfloat16"),
+    "G": ("sbuf", [128, 2048], "bfloat16"),
+    "GQ": ("sbuf", [128, 512], MX4), "GS": ("sbuf", [128, 512], "uint8"),
+    "LAQ": ("sbuf", [128, 256], MX4), "LAS": ("sbuf", [128, 256], "uint8"),
+    "LBQ": ("sbuf", [128, 192], MX4), "LBS": ("sbuf", [128, 192], "uint8"),
+    "IV": ("sbuf", [128, 32], "bfloat16"), "IF": ("sbuf", [128, 32], "float32"),
+    "IXD": ("dram", [8, 128, 1], "float32"), "IXL": ("dram", [8, 128, 1], "float32"),
+    "Y": ("sbuf", [128, 1024], "float32"),
+    "SB0": ("psum", [128, 512], "float32"), "SB1": ("psum", [128, 512], "float32"),
+    "SC0": ("psum", [128, 512], "float32"), "SC1": ("psum", [128, 512], "float32"),
+    "SC2": ("psum", [128, 512], "float32"), "SC3": ("psum", [128, 512], "float32"),
+}
+NEV = 100
+SEMAPHORES = ["arrA", "arrB", "arrX", "sent"] + ["e%d" % i for i in range(NEV)]
+MAGIC = 1.5 * 2.0 ** 27
+
+
+def rank_program(g, core, T, topo):
+    r = T.rank_of(core)
+    if r is None:
+        return
+    add, sub, mult = AluOpType.add, AluOpType.subtract, AluOpType.mult
+    ge, gt, eq = AluOpType.is_ge, AluOpType.is_gt, AluOpType.is_equal
+    Copy = ActivationFunctionType.Copy
+    v, s, te, sy = g.vector, g.scalar, g.tensor, g.sync
+    Q = {"g": g, "v": v, "s": s, "t": te, "y": sy}
+    events, seen, done = [], set(), set()
+
+    def ev():
+        h = [len(events), 0]
+        events.append(h)
+        return h
+
+    def inc(h, ins, n=1):
+        ins.then_inc(T.sem["e%d" % h[0]], n)
+        h[1] += n
+        return h
+
+    def one(ins, n=1):
+        return inc(ev(), ins, n)
+
+    def need(q, *hs):
+        for h in hs:
+            if (q, h[0]) not in seen:
+                seen.add((q, h[0]))
+                done.add(h[0])
+                Q[q].wait_ge(T.sem["e%d" % h[0]], h[1])
+
+    hx = [None] * 4
+    hu = one(sy.dma_start(T.UB[:], T.u[:, 0:16]), 16)
+    for a in range(4):
+        q = s if a % 2 == 0 else sy
+        hx[a] = one(q.dma_start(T.XB[:, 512 * a:512 * a + 512], T.x[:, 512 * a:512 * a + 512]), 16)
+    need("y", *hx)
+    hw = one(sy.dma_start(T.WB[:], T.w[:]), 16)
+
+    hpi = one(g.iota(T.PI[:], [[0, 32]], 0, 1))
+    hjf = one(g.iota(T.JF[:], [[128, 4], [0, 2], [1, 16]], -256, 0, allow_small_or_imprecise_dtypes=True))
+    hone = one(v.memset(T.ONE[:], 1.0))
+    need("g", hone)
+    hmk = one(g.affine_select(T.MK[:], T.ONE[:], [[1, 128]], ge, 0.0, 0, -1))
+    need("v", hpi)
+    hui = one(v.tensor_scalar(T.UI[:], T.PI[:], 3, None, AluOpType.bitwise_and))
+    hgi = one(v.tensor_scalar(T.GI[:, 0:1], T.PI[:, 0:1], 112, None, AluOpType.bitwise_and))
+    need("v", hui)
+    huo = one(v.tensor_copy(T.UO[:], T.UI[:]))
+    need("v", hgi)
+    hgf = one(v.tensor_copy(T.GF[:, 0:1], T.GI[:, 0:1]))
+    hsw = one(v.memset(T.SW[:], 0.0))
+    need("v", hgf, hjf)
+    hj = one(v.tensor_scalar(T.J[:], T.JF[:], T.GF[:, 0:1], None, add))
+    need("s", huo, hu)
+    hur1 = one(s.activation(T.UR[:, 256:512], T.UB[:, 0:16].indirect(T.UO[:, 16:32]), Copy))
+    need("v", huo, hu)
+    hur0 = one(v.tensor_copy(T.UR[:, 0:256], T.UB[:, 0:16].indirect(T.UO[:, 0:16])))
+
+    hq, hsc, hsb = [None] * 4, [None] * 4, [None] * 2
+    huq = ev()
+
+    def quant_x(a):
+        need("v", hx[a])
+        hq[a] = one(v.quantize_mx(T.XQ[:, 128 * a:128 * a + 128], T.XS[:, 128 * a:128 * a + 128],
+                                  T.XB[:, 512 * a:512 * a + 512]))
+
+    def score_col(a):
+        need("t", huq, hq[a])
+        hsc[a] = one(te.matmul_mx(T["SC%d" % a][:, 0:128], T.XQ[:, 128 * a:128 * a + 128],
+                                  T.XS[:, 128 * a:128 * a + 128], T.UQ[:], T.US[:], True, True))
+
+    def score_row(b):
+        need("t", huq, hq[2 * b], hq[2 * b + 1])
+        hsb[b] = one(te.matmul_mx(T["SB%d" % b][:, 0:256], T.UQ[:], T.US[:], T.XQ[:, 256 * b:256 * b + 256],
+                                  T.XS[:, 256 * b:256 * b + 256], True, True))
+
+    hc = [ev() for a in range(4)]
+    heq = [None] * 4
+
+    def compare(a, k0, k1, op):
+        b = k0 // 256
+        need("v", hsb[b], hsc[a])
+        inc(hc[a], v.tensor_scalar(T.C[:, 640 * a + 128 + k0:640 * a + 128 + k1],
+                                   T["SB%d" % b][:, k0 - 256 * b:k1 - 256 * b], T["SC%d" % a][:, 0:1], None, op))
+
+    def equals(a):
+        b, k = a // 2, 128 * (a % 2)
+        need("v", hsb[b], hsc[a])
+        heq[a] = one(v.tensor_scalar(T.EQ[:, 128 * a:128 * a + 128], T["SB%d" % b][:, k:k + 128],
+                                     T["SC%d" % a][:, 0:1], -1.0, eq, mult))
+
+    def late_equals(a):
+        need("v", heq[a], hmk)
+        inc(hc[a], v.tensor_tensor_scan(T.C[:, 640 * a:640 * a + 128], T.EQ[:, 128 * a:128 * a + 128], T.MK[:],
+                                        0.0, add, mult))
+
+    hcnt = [None] * 4
+
+    def total(a):
+        need("s", hc[a])
+        hcnt[a] = one(s.activation(T.JK[:, 520 * a:520 * a + 513], T.C[:, 640 * a + 127:640 * a + 640], Copy,
+                                   accum_out=T.CNT[:, 258 - a:259 - a]))
+
+    hpl = [None] * 4
+
+    def plane(q, e):
+        need(q, *hx)
+        out, inp = T.PL[:, 512 * e:512 * e + 512], T.XB[:, e:2048:4]
+        hpl[e] = one(v.tensor_copy(out, inp) if q == "v" else s.activation(out, inp, Copy))
+
+    plane("s", 2); plane("s", 3)
+    quant_x(0)
+    need("v", hur0, hur1)
+    inc(huq, v.quantize_mx(T.UQ[:], T.US[:], T.UR[:]))
+    score_col(0)
+    quant_x(1); score_row(0); score_col(1)
+    quant_x(2); score_col(2)
+    equals(0); compare(0, 0, 128, ge); compare(0, 128, 256, gt)
+    quant_x(3); score_row(1); score_col(3)
+    equals(1); late_equals(0); compare(1, 0, 256, ge); late_equals(1)
+    compare(0, 256, 512, gt); total(0)
+    compare(1, 256, 512, gt); total(1)
+    equals(2); compare(2, 0, 256, ge); compare(2, 256, 384, ge); late_equals(2); compare(2, 384, 512, gt); total(2)
+    equals(3); compare(3, 0, 256, ge); late_equals(3); compare(3, 256, 512, ge)
+
+    hof = ev()
+
+    def round16(i, c):
+        h = ev()
+        inc(h, v.tensor_scalar(T.XM[:, i:i + 2], T.CNT[:, c:c + 2], -7.5, MAGIC, add, add))
+        inc(h, v.tensor_scalar(T.XM[:, i + 4:i + 6], T.CNT[:, c:c + 2], 8.5, MAGIC, add, add))
+        return h
+
+    def offset(i, c, a):
+        inc(hof, v.tensor_scalar(T.OF[:, 2 * a:2 * a + 2], T.XM[:, i:8:4], MAGIC, T.CNT[:, c:c + 1], sub, add))
+
+    need("v", hcnt[0], hcnt[1])
+    h01 = round16(0, 257)
+    need("v", hc[3])
+    hcnt[3] = one(v.tensor_tensor_scan(T.CNT[:, 0:256], T.C[:, 2048:2304], T.C[:, 2304:2560], T.C[:, 2047:2048], add, add))
+    need("v", h01)
+    offset(0, 257, 1); offset(1, 258, 0)
+    need("v", hcnt[2], hcnt[3])
+    h23 = round16(2, 255)
+    need("v", h23)
+    offset(2, 255, 3); offset(3, 256, 2)
+
+    need("v", hof, hsw, hj)
+    h = one(v.tensor_copy(T.SW[:, 0:1024].indirect(T.OF[:, 0:8]), T.J[:]))
+    need("v", h)
+    h = one(v.transpose(T.TT[:], T.SW[:]))
+    need("v", h)
+    hz = one(v.tensor_tensor(T.Z[:, 0:32], T.TT[:, 0:1024:32], T.TT[:, 16:1024:32], add))
+    hzd = ev()
+    need("y", hz)
+    need("s", hz)
+    for k in (1, 2, 3):
+        m = 32 * k
+        inc(hzd, sy.dma_start(T.Z[0:128 - m, m:m + 32], T.Z[m:128, 0:32]), 16)
+        inc(hzd, s.dma_start(T.Z[128 - m:128, m:m + 32], T.Z[0:m, 0:32]), 16)
+    plane("v", 0); plane("v", 1)
+    need("v", hzd)
+    h = one(v.tensor_tensor(T.HA[:], T.Z[:, 0:64], T.Z[:, 64:128], add))
+    need("v", h)
+    hhb = one(v.tensor_tensor(T.HB[:], T.HA[:, 0:32], T.HA[:, 32:64], add))
+    need("v", hhb)
+    hot = one(v.tensor_scalar(T.OT[:], T.HB[:], 256.0, None, add))
+
+    def gather(q, run, n, e):
+        need(q, hot, hpl[e])
+        out = T.G[:, 256 * run + e:256 * (run + n):4]
+        win = T.PL[:, 512 * e:512 * e + 512].indirect(T.OT[:, 4 * run:4 * (run + n)])
+        return v.tensor_copy(out, win) if q == "v" else s.activation(out, win, Copy)
+
+    def gather_runs(run, n):
+        hv, hs = ev(), ev()
+        for e in (0, 1):
+            inc(hv, gather("v", run, n, e))
+        for e in (2, 3):
+            inc(hs, gather("s", run, n, e))
+        return hv, hs
+
+    def quant_runs(run, n, hv, hs):
+        need("v", hv, hs)
+        return one(v.quantize_mx(T.GQ[:, CH * run:CH * (run + n)], T.GS[:, CH * run:CH * (run + n)],
+                                 T.G[:, 256 * run:256 * (run + n)]))
+
+    own = r // 4
+    oth = 1 - own
+    first, second = 2 * ((r // 2) ^ 3), 2 * ((r // 2) ^ 2)
+    hv, hs = gather_runs(first, 2)
+    hiv = one(v.transpose(T.IV[:], T.HB[:]))
+    hq1 = quant_runs(first, 2, hv, hs)
+    need("v", hiv)
+    hif = one(v.tensor_scalar(T.IF[:], T.IV[:], 256.0, None, add))
+    hq2 = quant_runs(second, 2, *gather_runs(second, 2))
+    hq3 = quant_runs(4 * own, 4, *gather_runs(4 * own, 4))
+    need("v", hw)
+    hwq = one(v.quantize_mx(T.WQ[:], T.WS[:], T.WB[:]))
+
+    nsent = [0]
+    dt_u8 = T.XS.dtype
+
+    def fused(parts, sem):
+        ts = []
+        for d, eng, src, dst in parts:
+            rid, pid, _se = topo.addr(T.cores[d])
+            ts.append(RemoteDMATransfer(dst_ids=[DstId(rid=rid, pnc=pid)], dma_engine_mask=sum(1 << e for e in eng),
+                                        remote_sem=sem, src=src, dst=dst))
+            nsent[0] += len(eng)
+        g.remote_dma_fused(ts, local_sem=T.sem.sent)
+
+    def codes(buf, c):
+        return buf[:, c:c + CH].bitcast(dt_u8)
+
+    la = CH * (r % 4)
+    ps, far = [], []
+    for hqk, pair in ((hq1, first), (hq2, second)):
+        need("g", hqk)
+        pc = []
+        for i in range(2):
+            d = pair + i
+            e = topo.engines(core, T.cores[d])
+            w = len(e) // 2
+            pc.append((d, e[w * i:w * i + w], codes(T.GQ, CH * d), codes(T.LAQ, la)))
+            w = len(e) // 4
+            j = len(ps)
+            ps.append((d, e[w * j:w * j + w], T.GS[:, CH * d:CH * d + CH], T.LAS[:, la:la + CH]))
+            far.append(d)
+        fused(pc, T.sem.arrA)
+    fused(ps, T.sem.arrA)
+    need("g", hq3)
+    near = [r ^ k for k in (3, 1, 2)]
+    pc, ps = [], []
+    for i, d in enumerate(near):
+        e = topo.engines(core, T.cores[d])
+        w = len(e) // 4
+        cut = [e[0:w], e[w:2 * w], e[2 * w:]]
+        alt = [e[2 * w:3 * w], e[3 * w:], e[0:2 * w]]
+        slot = CH * ((r % 4) - (1 if r % 4 > d % 4 else 0))
+        pc.append((d, cut[i], codes(T.GQ, CH * d), codes(T.LBQ, slot)))
+        ps.append((d, alt[i], T.GS[:, CH * d:CH * d + CH], T.LBS[:, slot:slot + CH]))
+    fused(pc, T.sem.arrB)
+    fused(ps, T.sem.arrB)
+
+    need("y", hif)
+    hid = ev()
+    inc(hid, sy.dma_start(T.IXD[:, 0:64, 0], T.IF[0:32, 0:16]), 16)
+    inc(hid, sy.dma_start(T.IXD[:, 64:128, 0], T.IF[0:32, 16:32]), 16)
+    one(sy.dma_start(T.ix[r:r + 1, :], T.IF[4 * r:4 * r + 4, 0:16]), 16)
+    need("g", hid)
+    fused([(d, topo.engines(core, T.cores[d])[i:i + 1], T.IXD[d], T.IXL[r]) for i, d in enumerate(far + near)], T.sem.arrX)
+
+    def product(bank, o, q, sc):
+        return te.matmul_mx(bank, T.WQ[:, 128 * o:128 * o + 128], T.WS[:, 128 * o:128 * o + 128], q, sc, True, True)
+
+    def take(src, o, c, bank, h):
+        out = T.Y[:, (2 * src + o) * CH:(2 * src + o) * CH + CH]
+        inp = bank[:, c:c + CH]
+        inc(h, v.tensor_copy(out, inp) if o == 0 else s.activation(out, inp, Copy))
+
+    def finish(srcs, cols, banks, q, sc, n):
+        hp = [one(product(banks[o][:, 0:n], o, q, sc)) for o in range(O)]
+        hv, hs = ev(), ev()
+        need("v", hp[0])
+        need("s", hp[1])
+        for src, c in zip(srcs, cols):
+            take(src, 0, c, banks[0], hv)
+            take(src, 1, c, banks[1], hs)
+        return hv, hs
+
+    hy = ev()
+    need("t", hwq, hq3)
+    p0 = CH * (r - r % 2)
+    hv, hs = finish([r], [CH * (r % 2)], (T.SB0, T.SB1), T.GQ[:, p0:p0 + 128], T.GS[:, p0:p0 + 128], 128)
+    need("y", hv, hs)
+    one(sy.dma_start(T.y[:, 128 * r:128 * r + 128], T.Y[:, 128 * r:128 * r + 128]), 16)
+
+    te.wait_ge(T.sem.arrA, 24)
+    hv, hs = finish([4 * oth + i for i in range(4)], [CH * i for i in range(4)], (T.SC0, T.SC1), T.LAQ[:], T.LAS[:], 256)
+    need("y", hv, hs)
+    one(sy.dma_start(T.y[:, 512 * oth:512 * oth + 512], T.Y[:, 512 * oth:512 * oth + 512]), 16)
+
+    te.wait_ge(T.sem.arrB, 16)
+    rest = [4 * own + i for i in range(4) if 4 * own + i != r]
+    hv, hs = finish(rest, [CH * i for i in range(3)], (T.SC2, T.SC3), T.LBQ[:], T.LBS[:], 192)
+    lo, hi = (512 * own, 128 * r), (128 * r + 128, 512 * own + 512)
+    need("y", hv, hs)
+    if lo[0] < lo[1]:
+        inc(hy, sy.dma_start(T.y[:, lo[0]:lo[1]], T.Y[:, lo[0]:lo[1]]), 16)
+    if hi[0] < hi[1]:
+        need("s", hv, hs)
+        inc(hy, s.dma_start(T.y[:, hi[0]:hi[1]], T.Y[:, hi[0]:hi[1]]), 16)
+    s.wait_ge(T.sem.arrX, 7)
+    for a, b in ((0, r), (r + 1, N)):
+        if a < b:
+            inc(hy, s.dma_start(T.ix[a:b, :], T.IXL[a:b, 0:64, 0]), 16)
+
+    g.wait_ge(T.sem.sent, nsent[0])
+    for h in events:
+        if h[0] not in done and h[1]:
+            need("g", h)

@@ -3,6 +3,7 @@ from concourse.mybir import AluOpType, ActivationFunctionType
 
 N, TC, O, CH = 8, 512, 2, 64
 MX4 = "float8_e4m3fn_x4"
+AW, MW, QW = 384, 258, 264
 SCRATCH = {
     "UB": ("sbuf", [128, 16], "bfloat16"),
     "UR": ("sbuf", [128, 512], "bfloat16"),
@@ -15,29 +16,33 @@ SCRATCH = {
     "UI": ("sbuf", [128, 32], "int32"), "UO": ("sbuf", [128, 32], "uint16"),
     "GI": ("sbuf", [128, 8], "int32"), "GF": ("sbuf", [128, 8], "float32"),
     "JF": ("sbuf", [128, 128], "float32"), "J": ("sbuf", [128, 128], "bfloat16"),
-    "ONE": ("sbuf", [128, 128], "bfloat16"), "MK": ("sbuf", [128, 128], "bfloat16"),
-    "C": ("sbuf", [128, 2560], "bfloat16"),
-    "EQ": ("sbuf", [128, 512], "bfloat16"),
-    "JK": ("sbuf", [128, 1560], "bfloat16"),
-    "CNT": ("sbuf", [128, 264], "float32"),
+    "ONE": ("sbuf", [128, MW], "bfloat16"), "MK": ("sbuf", [128, 2 * MW], "bfloat16"),
+    "SCS": ("sbuf", [128, 4], "float32"),
+    "C": ("sbuf", [128, 1024], "bfloat16"),
+    "SG": ("sbuf", [128, 1024], "bfloat16"),
+    "AB": ("sbuf", [128, 4 * AW], "bfloat16"),
+    "AC": ("sbuf", [128, 4], "float32"),
+    "QS": ("sbuf", [128, 4 * QW], "bfloat16"),
+    "PK": ("sbuf", [128, 2], "float32"), "KK": ("sbuf", [128, 2], "float32"),
     "XM": ("sbuf", [128, 8], "float32"), "OF": ("sbuf", [128, 8], "uint16"),
     "SW": ("sbuf", [128, 1024], "bfloat16"), "TT": ("sbuf", [128, 1024], "bfloat16"),
     "Z": ("sbuf", [128, 128], "bfloat16"), "HA": ("sbuf", [128, 64], "bfloat16"), "HB": ("sbuf", [128, 32], "bfloat16"),
     "OT": ("sbuf", [128, 32], "uint16"),
     "PL": ("sbuf", [128, 2048], "bfloat16"),
     "G": ("sbuf", [128, 2048], "bfloat16"),
-    "GQ": ("sbuf", [128, 512], MX4), "GS": ("sbuf", [128, 512], "uint8"),
+    "GQ": ("sbuf", [128, 640], MX4), "GS": ("sbuf", [128, 640], "uint8"),
     "LAQ": ("sbuf", [128, 256], MX4), "LAS": ("sbuf", [128, 256], "uint8"),
     "LBQ": ("sbuf", [128, 192], MX4), "LBS": ("sbuf", [128, 192], "uint8"),
     "IV": ("sbuf", [128, 32], "bfloat16"), "IF": ("sbuf", [128, 32], "float32"),
-    "IXD": ("dram", [8, 128, 1], "float32"), "IXL": ("dram", [8, 128, 1], "float32"),
+    "ZT": ("sbuf", [128, 32], "bfloat16"), "ZF": ("sbuf", [128, 16], "float32"),
+    "IXD": ("dram", [2048, 1], "float32"), "IXL": ("dram", [8, 128, 1], "float32"),
     "Y": ("sbuf", [128, 1024], "float32"),
+    "VB0": ("psum", [128, 512], "float32"), "VB1": ("psum", [128, 512], "float32"),
     "SB0": ("psum", [128, 512], "float32"), "SB1": ("psum", [128, 512], "float32"),
-    "SC0": ("psum", [128, 512], "float32"), "SC1": ("psum", [128, 512], "float32"),
-    "SC2": ("psum", [128, 512], "float32"), "SC3": ("psum", [128, 512], "float32"),
+    "SC": ("psum", [128, 2048], "float32"),
 }
-NEV = 100
-SEMAPHORES = ["arrA", "arrB", "arrX", "sent"] + ["e%d" % i for i in range(NEV)]
+NEV = 140
+SEMAPHORES = ["arrA", "arrB", "arrC", "arrX", "sent"] + ["e%d" % i for i in range(NEV)]
 MAGIC = 1.5 * 2.0 ** 27
 
 
@@ -46,8 +51,9 @@ def rank_program(g, core, T, topo):
     if r is None:
         return
     add, sub, mult = AluOpType.add, AluOpType.subtract, AluOpType.mult
-    ge, gt, eq = AluOpType.is_ge, AluOpType.is_gt, AluOpType.is_equal
-    Copy = ActivationFunctionType.Copy
+    ge, gt = AluOpType.is_ge, AluOpType.is_gt
+    F = ActivationFunctionType
+    Copy = F.Copy
     v, s, te, sy = g.vector, g.scalar, g.tensor, g.sync
     Q = {"g": g, "v": v, "s": s, "t": te, "y": sy}
     events, seen, done = [], set(), set()
@@ -80,11 +86,22 @@ def rank_program(g, core, T, topo):
     need("y", *hx)
     hw = one(sy.dma_start(T.WB[:], T.w[:]), 16)
 
+    def iota(out, pattern, base, step=0):
+        return g.iota(out, pattern, base, step, allow_small_or_imprecise_dtypes=True)
+
     hpi = one(g.iota(T.PI[:], [[0, 32]], 0, 1))
-    hjf = one(g.iota(T.JF[:], [[128, 4], [0, 2], [1, 16]], -256, 0, allow_small_or_imprecise_dtypes=True))
     hone = one(v.memset(T.ONE[:], 1.0))
+    hkk = ev()
+    inc(hkk, v.memset(T.KK[:, 0:1], 248.5))
+    inc(hkk, v.memset(T.KK[:, 1:2], 264.5))
+    hjf = one(iota(T.JF[:], [[128, 4], [0, 2], [1, 16]], -256))
+    hpk = one(iota(T.PK[:], [[-256, 2]], 512, -2))
     need("g", hone)
-    hmk = one(g.affine_select(T.MK[:], T.ONE[:], [[1, 128]], ge, 0.0, 0, -1))
+    hm = ev()
+    for b in range(2):
+        inc(hm, g.affine_select(T.MK[:, MW * b:MW * b + MW], T.ONE[:], [[1, MW]], AluOpType.not_equal, -1.0,
+                                -1 - 128 * b, -1))
+    hsw = one(iota(T.SW[:], [[0, 1024]], 0))
     need("v", hpi)
     hui = one(v.tensor_scalar(T.UI[:], T.PI[:], 3, None, AluOpType.bitwise_and))
     hgi = one(v.tensor_scalar(T.GI[:, 0:1], T.PI[:, 0:1], 112, None, AluOpType.bitwise_and))
@@ -92,15 +109,14 @@ def rank_program(g, core, T, topo):
     huo = one(v.tensor_copy(T.UO[:], T.UI[:]))
     need("v", hgi)
     hgf = one(v.tensor_copy(T.GF[:, 0:1], T.GI[:, 0:1]))
-    hsw = one(v.memset(T.SW[:], 0.0))
-    need("v", hgf, hjf)
-    hj = one(v.tensor_scalar(T.J[:], T.JF[:], T.GF[:, 0:1], None, add))
+    need("s", hgf, hjf)
+    hj = one(s.activation(T.J[:], T.JF[:], F.Identity, bias=T.GF[:, 0:1]))
     need("s", huo, hu)
-    hur1 = one(s.activation(T.UR[:, 256:512], T.UB[:, 0:16].indirect(T.UO[:, 16:32]), Copy))
+    hur1 = one(s.activation(T.UR[:, 224:512], T.UB[:, 0:16].indirect(T.UO[:, 14:32]), Copy))
     need("v", huo, hu)
-    hur0 = one(v.tensor_copy(T.UR[:, 0:256], T.UB[:, 0:16].indirect(T.UO[:, 0:16])))
+    hur0 = one(v.tensor_copy(T.UR[:, 0:224], T.UB[:, 0:16].indirect(T.UO[:, 0:14])))
 
-    hq, hsc, hsb = [None] * 4, [None] * 4, [None] * 2
+    hq, hsc, hvb, hsb, hcol = [None] * 4, [None] * 4, [None] * 2, [None] * 2, [None] * 2
     huq = ev()
 
     def quant_x(a):
@@ -110,87 +126,93 @@ def rank_program(g, core, T, topo):
 
     def score_col(a):
         need("t", huq, hq[a])
-        hsc[a] = one(te.matmul_mx(T["SC%d" % a][:, 0:128], T.XQ[:, 128 * a:128 * a + 128],
+        hsc[a] = one(te.matmul_mx(T.SC[:, 512 * a:512 * a + 128], T.XQ[:, 128 * a:128 * a + 128],
                                   T.XS[:, 128 * a:128 * a + 128], T.UQ[:], T.US[:], True, True))
 
-    def score_row(b):
+    def score_row(bank, b):
         need("t", huq, hq[2 * b], hq[2 * b + 1])
-        hsb[b] = one(te.matmul_mx(T["SB%d" % b][:, 0:256], T.UQ[:], T.US[:], T.XQ[:, 256 * b:256 * b + 256],
-                                  T.XS[:, 256 * b:256 * b + 256], True, True))
+        return one(te.matmul_mx(T[bank % b][:, 0:256], T.UQ[:], T.US[:], T.XQ[:, 256 * b:256 * b + 256],
+                                T.XS[:, 256 * b:256 * b + 256], True, True))
 
-    hc = [ev() for a in range(4)]
-    heq = [None] * 4
+    hsg, hab, hcmp, htot, hpos, hxm = {}, {}, {}, {}, {}, {}
 
-    def compare(a, k0, k1, op):
-        b = k0 // 256
-        need("v", hsb[b], hsc[a])
-        inc(hc[a], v.tensor_scalar(T.C[:, 640 * a + 128 + k0:640 * a + 128 + k1],
-                                   T["SB%d" % b][:, k0 - 256 * b:k1 - 256 * b], T["SC%d" % a][:, 0:1], None, op))
+    def keep(b, *hs):
+        need("s", hsc[2 * b], hsc[2 * b + 1], *hs)
+        hcol[b] = one(s.activation(T.SCS[:, 2 * b:2 * b + 2], T.SC[:, 1024 * b:1024 * b + 1024:512], Copy))
 
-    def equals(a):
-        b, k = a // 2, 128 * (a % 2)
-        need("v", hsb[b], hsc[a])
-        heq[a] = one(v.tensor_scalar(T.EQ[:, 128 * a:128 * a + 128], T["SB%d" % b][:, k:k + 128],
-                                     T["SC%d" % a][:, 0:1], -1.0, eq, mult))
+    def signs(a):
+        b = a // 2
+        need("s", hcol[b], hsb[b])
+        hsg[a] = one(s.activation(T.SG[:, 256 * a:256 * a + 256], T["SB%d" % b][:, 0:256], F.Sign,
+                                  bias=T.SCS[:, a:a + 1], scale=-1.0, accum_out=T.AC[:, a:a + 1]))
 
-    def late_equals(a):
-        need("v", heq[a], hmk)
-        inc(hc[a], v.tensor_tensor_scan(T.C[:, 640 * a:640 * a + 128], T.EQ[:, 128 * a:128 * a + 128], T.MK[:],
-                                        0.0, add, mult))
+    def sizes(a):
+        need("s", hsg[a])
+        hab[a] = one(s.activation(T.AB[:, AW * a + 128:AW * a + 384], T.SG[:, 256 * a:256 * a + 256], F.Abs))
 
-    hcnt = [None] * 4
+    def compare(a):
+        b = 1 - a // 2
+        need("v", hvb[b], hsc[a] if b == 0 else hcol[0])
+        own = T.SC[:, 512 * a:512 * a + 1] if b == 0 else T.SCS[:, a:a + 1]
+        hcmp[a] = one(v.tensor_scalar(T.C[:, 256 * a:256 * a + 256], T["VB%d" % b][:, 0:256], own, -2.0,
+                                      gt if b else ge, mult))
 
     def total(a):
-        need("s", hc[a])
-        hcnt[a] = one(s.activation(T.JK[:, 520 * a:520 * a + 513], T.C[:, 640 * a + 127:640 * a + 640], Copy,
-                                   accum_out=T.CNT[:, 258 - a:259 - a]))
+        need("v", hcmp[a], hpk)
+        c = 256 * a
+        htot[a] = one(v.tensor_tensor_scan(T.AB[:, AW * a:AW * a + 128], T.C[:, c:c + 128], T.C[:, c + 128:c + 256],
+                                           T.PK[:, a % 2:a % 2 + 1], add, add))
 
-    hpl = [None] * 4
+    def late(a):
+        need("v", htot[a], hab[a], hmk)
+        m = MW * (a % 2)
+        hpos[a] = one(v.tensor_tensor_scan(T.QS[:, QW * a:QW * a + 257], T.AB[:, AW * a + 127:AW * a + 384],
+                                           T.MK[:, m:m + 257], T.AC[:, a:a + 1], add, mult))
 
-    def plane(q, e):
-        need(q, *hx)
-        out, inp = T.PL[:, 512 * e:512 * e + 512], T.XB[:, e:2048:4]
-        hpl[e] = one(v.tensor_copy(out, inp) if q == "v" else s.activation(out, inp, Copy))
+    def pos(a):
+        return T.QS[:, QW * a + 256:QW * a + 257]
 
-    plane("s", 2); plane("s", 3)
+    def round16(a):
+        need("v", hpos[a], hkk)
+        hxm[a] = one(v.tensor_scalar(T.XM[:, 2 * a:2 * a + 2], T.KK[:], pos(a), MAGIC, add, add))
+
+    hof = [ev(), ev()]
+
+    def offset(a):
+        need("v", hxm[a])
+        inc(hof[a // 2], v.tensor_scalar(T.OF[:, 2 * a:2 * a + 2], T.XM[:, 2 * a:2 * a + 2], MAGIC - 256.0, pos(a),
+                                         sub, add))
+
+    def scatter(b, *hs):
+        need("v", hof[b], hsw, hj, *hs)
+        return one(v.tensor_copy(T.SW[:, 0:1024].indirect(T.OF[:, 4 * b:4 * b + 4]), T.J[:, 64 * b:64 * b + 64]))
+
     quant_x(0)
     need("v", hur0, hur1)
     inc(huq, v.quantize_mx(T.UQ[:], T.US[:], T.UR[:]))
     score_col(0)
-    quant_x(1); score_row(0); score_col(1)
-    quant_x(2); score_col(2)
-    equals(0); compare(0, 0, 128, ge); compare(0, 128, 256, gt)
-    quant_x(3); score_row(1); score_col(3)
-    equals(1); late_equals(0); compare(1, 0, 256, ge); late_equals(1)
-    compare(0, 256, 512, gt); total(0)
-    compare(1, 256, 512, gt); total(1)
-    equals(2); compare(2, 0, 256, ge); compare(2, 256, 384, ge); late_equals(2); compare(2, 384, 512, gt); total(2)
-    equals(3); compare(3, 0, 256, ge); late_equals(3); compare(3, 256, 512, ge)
+    quant_x(1)
+    score_col(1)
+    hsb[0] = score_row("SB%d", 0)
+    hvb[0] = score_row("VB%d", 0)
+    quant_x(2)
+    score_col(2)
+    quant_x(3)
+    score_col(3)
+    hvb[1] = score_row("VB%d", 1)
+    hsb[1] = score_row("SB%d", 1)
+    need("v", hm)
+    hmk = one(v.tensor_scalar(T.MK[:, 256:2 * MW:MW], T.MK[:, 256:2 * MW:MW], 0.5, None, mult))
+    compare(2); compare(3)
+    keep(0); signs(0); signs(1); sizes(0); keep(1, hcmp[2], hcmp[3]); sizes(1)
+    signs(2); signs(3); sizes(2); sizes(3)
+    compare(0); compare(1); total(0); total(1); late(0); total(2); late(1); total(3)
+    round16(0); round16(1); offset(0); offset(1)
+    late(2)
+    h01 = scatter(0)
+    round16(2); late(3); offset(2); round16(3); offset(3)
 
-    hof = ev()
-
-    def round16(i, c):
-        h = ev()
-        inc(h, v.tensor_scalar(T.XM[:, i:i + 2], T.CNT[:, c:c + 2], -7.5, MAGIC, add, add))
-        inc(h, v.tensor_scalar(T.XM[:, i + 4:i + 6], T.CNT[:, c:c + 2], 8.5, MAGIC, add, add))
-        return h
-
-    def offset(i, c, a):
-        inc(hof, v.tensor_scalar(T.OF[:, 2 * a:2 * a + 2], T.XM[:, i:8:4], MAGIC, T.CNT[:, c:c + 1], sub, add))
-
-    need("v", hcnt[0], hcnt[1])
-    h01 = round16(0, 257)
-    need("v", hc[3])
-    hcnt[3] = one(v.tensor_tensor_scan(T.CNT[:, 0:256], T.C[:, 2048:2304], T.C[:, 2304:2560], T.C[:, 2047:2048], add, add))
-    need("v", h01)
-    offset(0, 257, 1); offset(1, 258, 0)
-    need("v", hcnt[2], hcnt[3])
-    h23 = round16(2, 255)
-    need("v", h23)
-    offset(2, 255, 3); offset(3, 256, 2)
-
-    need("v", hof, hsw, hj)
-    h = one(v.tensor_copy(T.SW[:, 0:1024].indirect(T.OF[:, 0:8]), T.J[:]))
+    h = scatter(1, h01)
     need("v", h)
     h = one(v.transpose(T.TT[:], T.SW[:]))
     need("v", h)
@@ -202,7 +224,25 @@ def rank_program(g, core, T, topo):
         m = 32 * k
         inc(hzd, sy.dma_start(T.Z[0:128 - m, m:m + 32], T.Z[m:128, 0:32]), 16)
         inc(hzd, s.dma_start(T.Z[128 - m:128, m:m + 32], T.Z[0:m, 0:32]), 16)
+
+    need("v", hz)
+    h = one(v.transpose(T.ZT[:], T.Z[:, 0:32]))
+    need("v", h)
+    h = one(v.tensor_scalar(T.ZF[:], T.ZT[:, 0:16], 64.0, None, add))
+    need("y", h)
+    hid = one(sy.dma_start(T.IXD[:, 0], T.ZF[:]), 16)
+
+    hpl = [None] * 4
+
+    def plane(q, e):
+        need(q, *hx)
+        out, inp = T.PL[:, 512 * e:512 * e + 512], T.XB[:, e:2048:4]
+        hpl[e] = one(v.tensor_copy(out, inp) if q == "v" else s.activation(out, inp, Copy))
+
+    plane("s", 3); plane("s", 2)
     plane("v", 0); plane("v", 1)
+    need("v", hw)
+    hwq = one(v.quantize_mx(T.WQ[:], T.WS[:], T.WB[:]))
     need("v", hzd)
     h = one(v.tensor_tensor(T.HA[:], T.Z[:, 0:64], T.Z[:, 64:128], add))
     need("v", h)
@@ -210,135 +250,107 @@ def rank_program(g, core, T, topo):
     need("v", hhb)
     hot = one(v.tensor_scalar(T.OT[:], T.HB[:], 256.0, None, add))
 
-    def gather(q, run, n, e):
-        need(q, hot, hpl[e])
-        out = T.G[:, 256 * run + e:256 * (run + n):4]
-        win = T.PL[:, 512 * e:512 * e + 512].indirect(T.OT[:, 4 * run:4 * (run + n)])
-        return v.tensor_copy(out, win) if q == "v" else s.activation(out, win, Copy)
+    def gather(q, h, run, n, slot, es):
+        for e in es:
+            need(q, hot, hpl[e])
+            out = T.G[:, 256 * slot + e:256 * (slot + n):4]
+            win = T.PL[:, 512 * e:512 * e + 512].indirect(T.OT[:, 4 * run:4 * (run + n)])
+            inc(h, v.tensor_copy(out, win) if q == "v" else s.activation(out, win, Copy))
+        return h
 
-    def gather_runs(run, n):
-        hv, hs = ev(), ev()
-        for e in (0, 1):
-            inc(hv, gather("v", run, n, e))
-        for e in (2, 3):
-            inc(hs, gather("s", run, n, e))
-        return hv, hs
+    def stage(run, n, slot, nv):
+        return gather("v", ev(), run, n, slot, range(nv)), gather("s", ev(), run, n, slot, range(nv, 4))
 
-    def quant_runs(run, n, hv, hs):
-        need("v", hv, hs)
-        return one(v.quantize_mx(T.GQ[:, CH * run:CH * (run + n)], T.GS[:, CH * run:CH * (run + n)],
-                                 T.G[:, 256 * run:256 * (run + n)]))
+    def quant(slot, c, hs):
+        need("v", *hs)
+        return one(v.quantize_mx(T.GQ[:, c:c + 128], T.GS[:, c:c + 128], T.G[:, 256 * slot:256 * slot + 512]))
 
-    own = r // 4
-    oth = 1 - own
-    first, second = 2 * ((r // 2) ^ 3), 2 * ((r // 2) ^ 2)
-    hv, hs = gather_runs(first, 2)
+    pairs = [2 * ((r // 2) ^ k) for k in (3, 2, 1)]
+    partner = r ^ 1
+    hq1 = quant(0, 0, stage(pairs[0], 2, 0, 2))
+    hq2 = quant(2, 128, stage(pairs[1], 2, 2, 2))
+    hq3 = quant(4, 256, stage(pairs[2], 2, 4, 2))
+    hq4 = quant(5, 384, stage(partner, 1, 6, 1))
+    hq5 = quant(6, 512, stage(r, 1, 7, 2))
     hiv = one(v.transpose(T.IV[:], T.HB[:]))
-    hq1 = quant_runs(first, 2, hv, hs)
     need("v", hiv)
     hif = one(v.tensor_scalar(T.IF[:], T.IV[:], 256.0, None, add))
-    hq2 = quant_runs(second, 2, *gather_runs(second, 2))
-    hq3 = quant_runs(4 * own, 4, *gather_runs(4 * own, 4))
-    need("v", hw)
-    hwq = one(v.quantize_mx(T.WQ[:], T.WS[:], T.WB[:]))
+    need("y", hif)
+    one(sy.dma_start(T.ix[r:r + 1, :], T.IF[4 * r:4 * r + 4, 0:16]), 16)
 
     nsent = [0]
     dt_u8 = T.XS.dtype
 
     def fused(parts, sem):
         ts = []
-        for d, eng, src, dst in parts:
+        for i, (d, src, dst) in enumerate(parts):
             rid, pid, _se = topo.addr(T.cores[d])
-            ts.append(RemoteDMATransfer(dst_ids=[DstId(rid=rid, pnc=pid)], dma_engine_mask=sum(1 << e for e in eng),
-                                        remote_sem=sem, src=src, dst=dst))
-            nsent[0] += len(eng)
+            e = topo.engines(core, T.cores[d])
+            w = len(e) // len(parts)
+            many = isinstance(src, list)
+            ts.append(RemoteDMATransfer(dst_ids=[DstId(rid=rid, pnc=pid)], dma_engine_mask=sum(1 << k for k in e[w * i:w * i + w]),
+                                        remote_sem=sem, srcs=src if many else [src], dsts=[dst], alu_op=int(many)))
+            nsent[0] += w
         g.remote_dma_fused(ts, local_sem=T.sem.sent)
 
     def codes(buf, c):
         return buf[:, c:c + CH].bitcast(dt_u8)
 
-    la = CH * (r % 4)
-    ps, far = [], []
-    for hqk, pair in ((hq1, first), (hq2, second)):
-        need("g", hqk)
-        pc = []
-        for i in range(2):
-            d = pair + i
-            e = topo.engines(core, T.cores[d])
-            w = len(e) // 2
-            pc.append((d, e[w * i:w * i + w], codes(T.GQ, CH * d), codes(T.LAQ, la)))
-            w = len(e) // 4
-            j = len(ps)
-            ps.append((d, e[w * j:w * j + w], T.GS[:, CH * d:CH * d + CH], T.LAS[:, la:la + CH]))
-            far.append(d)
-        fused(pc, T.sem.arrA)
-    fused(ps, T.sem.arrA)
-    need("g", hq3)
-    near = [r ^ k for k in (3, 1, 2)]
-    pc, ps = [], []
-    for i, d in enumerate(near):
-        e = topo.engines(core, T.cores[d])
-        w = len(e) // 4
-        cut = [e[0:w], e[w:2 * w], e[2 * w:]]
-        alt = [e[2 * w:3 * w], e[3 * w:], e[0:2 * w]]
-        slot = CH * ((r % 4) - (1 if r % 4 > d % 4 else 0))
-        pc.append((d, cut[i], codes(T.GQ, CH * d), codes(T.LBQ, slot)))
-        ps.append((d, alt[i], T.GS[:, CH * d:CH * d + CH], T.LBS[:, slot:slot + CH]))
-    fused(pc, T.sem.arrB)
-    fused(ps, T.sem.arrB)
+    def send_codes(ds, c, buf, at, sem):
+        fused([(d, codes(T.GQ, c + CH * i), codes(buf, at)) for i, d in enumerate(ds)], sem)
 
-    need("y", hif)
-    hid = ev()
-    inc(hid, sy.dma_start(T.IXD[:, 0:64, 0], T.IF[0:32, 0:16]), 16)
-    inc(hid, sy.dma_start(T.IXD[:, 64:128, 0], T.IF[0:32, 16:32]), 16)
-    one(sy.dma_start(T.ix[r:r + 1, :], T.IF[4 * r:4 * r + 4, 0:16]), 16)
+    def send_scales(ds, c, buf, at, sem):
+        fused([(d, T.GS[:, c + CH * i:c + CH * i + CH], buf[:, at:at + CH]) for i, d in enumerate(ds)], sem)
+
+    dA, dB, dC = [[p, p + 1] for p in pairs]
+    la, lb = CH * (r % 4), CH * (r % 2)
     need("g", hid)
-    fused([(d, topo.engines(core, T.cores[d])[i:i + 1], T.IXD[d], T.IXL[r]) for i, d in enumerate(far + near)], T.sem.arrX)
+    fused([(d, [T.IXD[512 * k + 128 * (d // 2):512 * k + 128 * (d // 2) + 128, :] for k in range(4)], T.IXL[r])
+           for d in dA + dB + dC + [partner]], T.sem.arrX)
+    need("g", hq1)
+    send_codes(dA, 0, T.LAQ, la, T.sem.arrA)
+    need("g", hq2)
+    send_codes(dB, 128, T.LAQ, la, T.sem.arrA)
+    send_scales(dA + dB, 0, T.LAS, la, T.sem.arrA)
+    need("g", hq3)
+    send_codes(dC, 256, T.LBQ, lb, T.sem.arrB)
+    send_scales(dC, 256, T.LBS, lb, T.sem.arrB)
+    need("g", hq4)
+    send_codes([partner], 448, T.LBQ, 128, T.sem.arrC)
+    send_scales([partner], 448, T.LBS, 128, T.sem.arrC)
 
     def product(bank, o, q, sc):
         return te.matmul_mx(bank, T.WQ[:, 128 * o:128 * o + 128], T.WS[:, 128 * o:128 * o + 128], q, sc, True, True)
 
-    def take(src, o, c, bank, h):
+    def take(src, o, inp, h):
         out = T.Y[:, (2 * src + o) * CH:(2 * src + o) * CH + CH]
-        inp = bank[:, c:c + CH]
         inc(h, v.tensor_copy(out, inp) if o == 0 else s.activation(out, inp, Copy))
 
-    def finish(srcs, cols, banks, q, sc, n):
-        hp = [one(product(banks[o][:, 0:n], o, q, sc)) for o in range(O)]
-        hv, hs = ev(), ev()
+    def finish(srcs, c0, banks, q, sc, n):
+        hp = [one(product(buf[:, at:at + n], o, q, sc)) for o, (buf, at) in enumerate(banks)]
+        hs = [ev(), ev()]
         need("v", hp[0])
         need("s", hp[1])
-        for src, c in zip(srcs, cols):
-            take(src, 0, c, banks[0], hv)
-            take(src, 1, c, banks[1], hs)
-        return hv, hs
+        for i, src in enumerate(srcs):
+            for o, (buf, at) in enumerate(banks):
+                take(src, o, buf[:, at + c0 + CH * i:at + c0 + CH * i + CH], hs[o])
+        need("y", *hs)
+        lo, hi = 128 * srcs[0], 128 * srcs[-1] + 128
+        one(sy.dma_start(T.y[:, lo:hi], T.Y[:, lo:hi]), 16)
 
-    hy = ev()
-    need("t", hwq, hq3)
-    p0 = CH * (r - r % 2)
-    hv, hs = finish([r], [CH * (r % 2)], (T.SB0, T.SB1), T.GQ[:, p0:p0 + 128], T.GS[:, p0:p0 + 128], 128)
-    need("y", hv, hs)
-    one(sy.dma_start(T.y[:, 128 * r:128 * r + 128], T.Y[:, 128 * r:128 * r + 128]), 16)
-
-    te.wait_ge(T.sem.arrA, 24)
-    hv, hs = finish([4 * oth + i for i in range(4)], [CH * i for i in range(4)], (T.SC0, T.SC1), T.LAQ[:], T.LAS[:], 256)
-    need("y", hv, hs)
-    one(sy.dma_start(T.y[:, 512 * oth:512 * oth + 512], T.Y[:, 512 * oth:512 * oth + 512]), 16)
-
-    te.wait_ge(T.sem.arrB, 16)
-    rest = [4 * own + i for i in range(4) if 4 * own + i != r]
-    hv, hs = finish(rest, [CH * i for i in range(3)], (T.SC2, T.SC3), T.LBQ[:], T.LBS[:], 192)
-    lo, hi = (512 * own, 128 * r), (128 * r + 128, 512 * own + 512)
-    need("y", hv, hs)
-    if lo[0] < lo[1]:
-        inc(hy, sy.dma_start(T.y[:, lo[0]:lo[1]], T.Y[:, lo[0]:lo[1]]), 16)
-    if hi[0] < hi[1]:
-        need("s", hv, hs)
-        inc(hy, s.dma_start(T.y[:, hi[0]:hi[1]], T.Y[:, hi[0]:hi[1]]), 16)
-    s.wait_ge(T.sem.arrX, 7)
+    need("t", hwq, hq5)
+    finish([r], CH, ((T.VB0, 0), (T.SB0, 0)), T.GQ[:, 512:640], T.GS[:, 512:640], 128)
+    sy.wait_ge(T.sem.arrX, 7)
     for a, b in ((0, r), (r + 1, N)):
         if a < b:
-            inc(hy, s.dma_start(T.ix[a:b, :], T.IXL[a:b, 0:64, 0]), 16)
+            one(sy.dma_start(T.ix[a:b, :], T.IXL[a:b, lb:lb + CH, 0]), 16)
+    te.wait_ge(T.sem.arrA, 24)
+    oth = 4 * (1 - r // 4)
+    finish(range(oth, oth + 4), 0, ((T.SC, 0), (T.SC, 512)), T.LAQ[:], T.LAS[:], 256)
+    te.wait_ge(T.sem.arrB, 16)
+    finish(dC, 0, ((T.SC, 1024), (T.SC, 1536)), T.LBQ[:, 0:128], T.LBS[:, 0:128], 128)
+    te.wait_ge(T.sem.arrC, 16)
+    finish([partner], CH, ((T.VB1, 0), (T.SB1, 0)), T.LBQ[:, 64:192], T.LBS[:, 64:192], 128)
 
     g.wait_ge(T.sem.sent, nsent[0])
     for h in events:

@@ -1,9 +1,9 @@
 from concourse.bass import DstId, RemoteDMATransfer
-from concourse.mybir import AluOpType, ActivationFunctionType
+from concourse.mybir import dt, AluOpType, ActivationFunctionType
 
 N, TC, O, CH = 8, 512, 2, 64
 MX4 = "float8_e4m3fn_x4"
-AW, MW, QW = 384, 258, 264
+AW, MW, QW = 392, 260, 264
 SCRATCH = {
     "UB": ("sbuf", [128, 16], "bfloat16"),
     "UR": ("sbuf", [128, 512], "bfloat16"),
@@ -24,31 +24,77 @@ SCRATCH = {
     "AC": ("sbuf", [128, 4], "float32"),
     "QS": ("sbuf", [128, 4 * QW], "bfloat16"),
     "PK": ("sbuf", [128, 2], "float32"), "KK": ("sbuf", [128, 2], "float32"),
-    "XM": ("sbuf", [128, 8], "float32"), "OF": ("sbuf", [128, 8], "uint16"),
+    "OF": ("sbuf", [128, 8], "uint16"),
     "SW": ("sbuf", [128, 1024], "bfloat16"), "TT": ("sbuf", [128, 1024], "bfloat16"),
     "Z": ("sbuf", [128, 128], "bfloat16"), "HA": ("sbuf", [128, 64], "bfloat16"), "HB": ("sbuf", [128, 32], "bfloat16"),
     "OT": ("sbuf", [128, 32], "uint16"),
     "PL": ("sbuf", [128, 2048], "bfloat16"),
-    "G": ("sbuf", [128, 2048], "bfloat16"),
-    "GQ": ("sbuf", [128, 640], MX4), "GS": ("sbuf", [128, 640], "uint8"),
+    "G": ("sbuf", [128, 2304], "bfloat16"),
+    "GQ": ("sbuf", [128, 768], MX4), "GS": ("sbuf", [128, 768], "uint8"),
     "LAQ": ("sbuf", [128, 256], MX4), "LAS": ("sbuf", [128, 256], "uint8"),
     "LBQ": ("sbuf", [128, 192], MX4), "LBS": ("sbuf", [128, 192], "uint8"),
-    "IV": ("sbuf", [128, 32], "bfloat16"), "IF": ("sbuf", [128, 32], "float32"),
-    "ZT": ("sbuf", [128, 32], "bfloat16"), "ZF": ("sbuf", [128, 16], "float32"),
-    "IXD": ("dram", [2048, 1], "float32"), "IXL": ("dram", [8, 128, 1], "float32"),
-    "Y": ("sbuf", [128, 1024], "float32"),
+    "HQ": ("sbuf", [128, CH], MX4), "HS": ("sbuf", [128, CH], "uint8"),
+    "IV": ("sbuf", [128, 32], "bfloat16"), "IF": ("sbuf", [128, 16], "float32"),
+    "NB": ("sbuf", [128, 4, 32], "bfloat16"), "NF": ("sbuf", [128, 4, 16], "float32"),
+    "IXD": ("dram", [8192, 1], "bfloat16"), "IXL": ("dram", [8, 128, 1], "bfloat16"),
+    "Y": ("sbuf", [128, N, O, CH], "float32"),
     "VB0": ("psum", [128, 512], "float32"), "VB1": ("psum", [128, 512], "float32"),
     "SB0": ("psum", [128, 512], "float32"), "SB1": ("psum", [128, 512], "float32"),
     "SC": ("psum", [128, 2048], "float32"),
 }
 NEV = 140
-SEMAPHORES = ["arrA", "arrB", "arrC", "arrX", "sent"] + ["e%d" % i for i in range(NEV)]
-MAGIC = 1.5 * 2.0 ** 27
+SEMAPHORES = ["arrA", "arrB", "arrC", "arrD", "arrH", "arrX", "sent"] + ["e%d" % i for i in range(NEV)]
+MAGIC = 2304.0
+
+
+HELPERS = 0
+
+
+def transfer(topo, to, mask, sem, src, dst):
+    rid, pid, _se = topo.addr(to)
+    many = isinstance(src, list)
+    return RemoteDMATransfer(dst_ids=[DstId(rid=rid, pnc=pid)], dma_engine_mask=mask, remote_sem=sem,
+                             srcs=src if many else [src], dsts=[dst], alu_op=int(many))
+
+
+def helpers_of(T, topo, r):
+    core = T.cores[r]
+    free = [c for c in topo.cores_of(core) if c != core and topo.die(c) == topo.die(core)]
+    out = []
+    for k, near in ((6, False), (4, True)):
+        d = [j for j in (r ^ k, r ^ k ^ 1) if topo.same_plane(topo.chip(core), topo.chip(T.cores[j])) == near][0]
+        h = [c for c in free if topo.may_write(c, T.cores[d])][0]
+        free.remove(h)
+        out.append((h, d))
+    return out[:HELPERS]
+
+
+def bits(engines):
+    return sum(1 << e for e in engines)
+
+
+def codes(buf, c):
+    return buf[:, c:c + CH].bitcast(dt.uint8)
+
+
+def scales(buf, c):
+    return buf[:, c:c + CH]
 
 
 def rank_program(g, core, T, topo):
     r = T.rank_of(core)
     if r is None:
+        for k in range(N):
+            for i, (helper, d) in enumerate(helpers_of(T, topo, k)):
+                if helper != core:
+                    continue
+                m, at, arr = topo.mask(core, T.cores[d]), CH * (k % 4), T.sem[("arrA", "arrD")[i]]
+                for got, n, sem, src, dst in ((T.sem.arrX, 8 // HELPERS, T.sem.arrX, T.IXL[k], T.IXL[k]),
+                                              (T.sem.arrA, 8, arr, codes(T.HQ, 0), codes(T.LAQ, at)),
+                                              (T.sem.arrB, 8, arr, scales(T.HS, 0), scales(T.LAS, at))):
+                    g.wait_ge(got, n)
+                    g.remote_dma_fused([transfer(topo, T.cores[d], m, sem, src, dst)], local_sem=T.sem.sent)
+                g.wait_ge(T.sem.sent, 24)
         return
     add, sub, mult = AluOpType.add, AluOpType.subtract, AluOpType.mult
     ge, gt = AluOpType.is_ge, AluOpType.is_gt
@@ -81,8 +127,7 @@ def rank_program(g, core, T, topo):
     hx = [None] * 4
     hu = one(sy.dma_start(T.UB[:], T.u[:, 0:16]), 16)
     for a in range(4):
-        q = s if a % 2 == 0 else sy
-        hx[a] = one(q.dma_start(T.XB[:, 512 * a:512 * a + 512], T.x[:, 512 * a:512 * a + 512]), 16)
+        hx[a] = one((sy if a % 2 else s).dma_start(T.XB[:, 512 * a:512 * a + 512], T.x[:, 512 * a:512 * a + 512]), 16)
     need("y", *hx)
     hw = one(sy.dma_start(T.WB[:], T.w[:]), 16)
 
@@ -92,8 +137,8 @@ def rank_program(g, core, T, topo):
     hpi = one(g.iota(T.PI[:], [[0, 32]], 0, 1))
     hone = one(v.memset(T.ONE[:], 1.0))
     hkk = ev()
-    inc(hkk, v.memset(T.KK[:, 0:1], 248.5))
-    inc(hkk, v.memset(T.KK[:, 1:2], 264.5))
+    inc(hkk, v.memset(T.KK[:, 0:1], 256.0 - MAGIC))
+    inc(hkk, v.memset(T.KK[:, 1:2], 272.0 - MAGIC))
     hjf = one(iota(T.JF[:], [[128, 4], [0, 2], [1, 16]], -256))
     hpk = one(iota(T.PK[:], [[-256, 2]], 512, -2))
     need("g", hone)
@@ -109,6 +154,9 @@ def rank_program(g, core, T, topo):
     huo = one(v.tensor_copy(T.UO[:], T.UI[:]))
     need("v", hgi)
     hgf = one(v.tensor_copy(T.GF[:, 0:1], T.GI[:, 0:1]))
+    inc(hkk, v.memset(T.AB[:, 384:4 * AW:AW], MAGIC + 256.0))
+    inc(hkk, v.memset(T.AB[:, 385:4 * AW:AW], -7.5))
+    hnz = one(v.memset(T.NB[0:N], 0.0))
     need("s", hgf, hjf)
     hj = one(s.activation(T.J[:], T.JF[:], F.Identity, bias=T.GF[:, 0:1]))
     need("s", huo, hu)
@@ -164,24 +212,20 @@ def rank_program(g, core, T, topo):
                                            T.PK[:, a % 2:a % 2 + 1], add, add))
 
     def late(a):
-        need("v", htot[a], hab[a], hmk)
+        need("v", htot[a], hab[a], hmk, hkk)
         m = MW * (a % 2)
-        hpos[a] = one(v.tensor_tensor_scan(T.QS[:, QW * a:QW * a + 257], T.AB[:, AW * a + 127:AW * a + 384],
-                                           T.MK[:, m:m + 257], T.AC[:, a:a + 1], add, mult))
+        hpos[a] = one(v.tensor_tensor_scan(T.QS[:, QW * a:QW * a + 259], T.AB[:, AW * a + 127:AW * a + 386],
+                                           T.MK[:, m:m + 259], T.AC[:, a:a + 1], add, mult))
 
     def pos(a):
         return T.QS[:, QW * a + 256:QW * a + 257]
 
-    def round16(a):
-        need("v", hpos[a], hkk)
-        hxm[a] = one(v.tensor_scalar(T.XM[:, 2 * a:2 * a + 2], T.KK[:], pos(a), MAGIC, add, add))
-
     hof = [ev(), ev()]
 
     def offset(a):
-        need("v", hxm[a])
-        inc(hof[a // 2], v.tensor_scalar(T.OF[:, 2 * a:2 * a + 2], T.XM[:, 2 * a:2 * a + 2], MAGIC - 256.0, pos(a),
-                                         sub, add))
+        need("v", hpos[a])
+        inc(hof[a // 2], v.tensor_scalar(T.OF[:, 2 * a:2 * a + 2], T.KK[:], T.QS[:, QW * a + 258:QW * a + 259], pos(a),
+                                         add, add))
 
     def scatter(b, *hs):
         need("v", hof[b], hsw, hj, *hs)
@@ -201,36 +245,44 @@ def rank_program(g, core, T, topo):
     score_col(3)
     hvb[1] = score_row("VB%d", 1)
     hsb[1] = score_row("SB%d", 1)
-    need("v", hm)
-    hmk = one(v.tensor_scalar(T.MK[:, 256:2 * MW:MW], T.MK[:, 256:2 * MW:MW], 0.5, None, mult))
     compare(2); compare(3)
+    need("s", hm)
+    hmk = one(s.activation(T.MK[:, 256:2 * MW:MW], T.MK[:, 256:2 * MW:MW], Copy, scale=0.5))
     keep(0); signs(0); signs(1); sizes(0); keep(1, hcmp[2], hcmp[3]); sizes(1)
     signs(2); signs(3); sizes(2); sizes(3)
-    compare(0); compare(1); total(0); total(1); late(0); total(2); late(1); total(3)
-    round16(0); round16(1); offset(0); offset(1)
-    late(2)
+    compare(0); compare(1); total(0); total(1); late(0); late(1); offset(0); total(2); offset(1); total(3)
     h01 = scatter(0)
-    round16(2); late(3); offset(2); round16(3); offset(3)
+    late(2); late(3); offset(2); offset(3)
 
     h = scatter(1, h01)
     need("v", h)
-    h = one(v.transpose(T.TT[:], T.SW[:]))
-    need("v", h)
-    hz = one(v.tensor_tensor(T.Z[:, 0:32], T.TT[:, 0:1024:32], T.TT[:, 16:1024:32], add))
-    hzd = ev()
-    need("y", hz)
-    need("s", hz)
-    for k in (1, 2, 3):
-        m = 32 * k
-        inc(hzd, sy.dma_start(T.Z[0:128 - m, m:m + 32], T.Z[m:128, 0:32]), 16)
-        inc(hzd, s.dma_start(T.Z[128 - m:128, m:m + 32], T.Z[0:m, 0:32]), 16)
+    hsc2 = h
+    own = r // 4
+    oth = 1 - own
+    htt, hz, hzd = {}, {}, {}
 
-    need("v", hz)
-    h = one(v.transpose(T.ZT[:], T.Z[:, 0:32]))
-    need("v", h)
-    h = one(v.tensor_scalar(T.ZF[:], T.ZT[:, 0:16], 64.0, None, add))
-    need("y", h)
-    hid = one(sy.dma_start(T.IXD[:, 0], T.ZF[:]), 16)
+    def turn(b):
+        htt[b] = one(v.transpose(T.TT[:, 512 * b:512 * b + 512], T.SW[:, 512 * b:512 * b + 512]))
+
+    def exchange(b, qs):
+        need("v", htt[b])
+        c = 512 * b
+        hz[b] = one(v.tensor_tensor(T.Z[:, 64 * b:64 * b + 16], T.TT[:, c:c + 512:32], T.TT[:, c + 16:c + 512:32], add))
+        hzd[b] = ev()
+        src = 64 * b
+        for k in (1, 2, 3):
+            m, dst = 32 * k, 64 * b + 16 * k
+            for qn, lo, hi, at in ((qs[0], 0, 128 - m, m), (qs[1], 128 - m, 128, 0)):
+                need(qn, hz[b])
+                inc(hzd[b], Q[qn].dma_start(T.Z[lo:hi, dst:dst + 16], T.Z[at:at + hi - lo, src:src + 16]), 16)
+
+    turn(oth)
+    exchange(oth, "ys")
+    need("y", hsc2)
+    hid = one(sy.dma_start(T.IXD[:, 0], T.SW[0:128:16, :]), 16)
+    turn(own)
+    exchange(own, "yy")
+
 
     hpl = [None] * 4
 
@@ -241,19 +293,26 @@ def rank_program(g, core, T, topo):
 
     plane("s", 3); plane("s", 2)
     plane("v", 0); plane("v", 1)
-    need("v", hw)
-    hwq = one(v.quantize_mx(T.WQ[:], T.WS[:], T.WB[:]))
-    need("v", hzd)
-    h = one(v.tensor_tensor(T.HA[:], T.Z[:, 0:64], T.Z[:, 64:128], add))
-    need("v", h)
-    hhb = one(v.tensor_tensor(T.HB[:], T.HA[:, 0:32], T.HA[:, 32:64], add))
-    need("v", hhb)
-    hot = one(v.tensor_scalar(T.OT[:], T.HB[:], 256.0, None, add))
+    hot = {}
+
+    def whole(b):
+        need("v", hzd[b])
+        h = one(v.tensor_tensor(T.HA[:, 32 * b:32 * b + 32], T.Z[:, 64 * b:64 * b + 32], T.Z[:, 64 * b + 32:64 * b + 64], add))
+        yield
+        need("v", h)
+        h = one(v.tensor_tensor(T.HB[:, 16 * b:16 * b + 16], T.HA[:, 32 * b:32 * b + 16], T.HA[:, 32 * b + 16:32 * b + 32], add))
+        yield
+        need("v", h)
+        hot[b] = one(v.tensor_scalar(T.OT[:, 16 * b:16 * b + 16], T.HB[:, 16 * b:16 * b + 16], 256.0, None, add))
+        yield
+
+    list(whole(oth))
+    later = whole(own)
 
     def gather(q, h, run, n, slot, es):
         for e in es:
-            need(q, hot, hpl[e])
-            out = T.G[:, 256 * slot + e:256 * (slot + n):4]
+            need(q, hot[run // 4], hpl[e])
+            out = T.G[:, 256 * (slot + 1) + e:256 * (slot + 1 + n):4]
             win = T.PL[:, 512 * e:512 * e + 512].indirect(T.OT[:, 4 * run:4 * (run + n)])
             inc(h, v.tensor_copy(out, win) if q == "v" else s.activation(out, win, Copy))
         return h
@@ -262,24 +321,28 @@ def rank_program(g, core, T, topo):
         return gather("v", ev(), run, n, slot, range(nv)), gather("s", ev(), run, n, slot, range(nv, 4))
 
     def quant(slot, c, hs):
-        need("v", *hs)
-        return one(v.quantize_mx(T.GQ[:, c:c + 128], T.GS[:, c:c + 128], T.G[:, 256 * slot:256 * slot + 512]))
+        need("v", *[h for h in hs if h[1]])
+        return one(v.quantize_mx(T.GQ[:, c:c + 128], T.GS[:, c:c + 128], T.G[:, 256 * slot + 256:256 * slot + 768]))
 
     pairs = [2 * ((r // 2) ^ k) for k in (3, 2, 1)]
     partner = r ^ 1
-    hq1 = quant(0, 0, stage(pairs[0], 2, 0, 2))
-    hq2 = quant(2, 128, stage(pairs[1], 2, 2, 2))
+    hA = stage(pairs[0], 2, 0, 2)
+    next(later)
+    hq1 = quant(0, 0, hA)
+    next(later)
+    hB = stage(pairs[1], 2, 2, 1)
+    next(later)
+    hq2 = quant(2, 128, hB)
     hq3 = quant(4, 256, stage(pairs[2], 2, 4, 2))
-    hq4 = quant(5, 384, stage(partner, 1, 6, 1))
-    hq5 = quant(6, 512, stage(r, 1, 7, 2))
+    hq4 = quant(5, 384, stage(partner, 1, 6, 0))
+    need("v", hw)
+    hwq = one(v.quantize_mx(T.WQ[:], T.WS[:], T.WB[:]))
+    hq5 = quant(6, 512, stage(r, 1, 7, 1))
     hiv = one(v.transpose(T.IV[:], T.HB[:]))
     need("v", hiv)
-    hif = one(v.tensor_scalar(T.IF[:], T.IV[:], 256.0, None, add))
-    need("y", hif)
-    one(sy.dma_start(T.ix[r:r + 1, :], T.IF[4 * r:4 * r + 4, 0:16]), 16)
+    hif = one(v.tensor_scalar(T.IF[:], T.IV[:, 0:16], 256.0, None, add))
 
     nsent = [0]
-    dt_u8 = T.XS.dtype
 
     def fused(parts, sem):
         ts = []
@@ -287,14 +350,12 @@ def rank_program(g, core, T, topo):
             rid, pid, _se = topo.addr(T.cores[d])
             e = topo.engines(core, T.cores[d])
             w = len(e) // len(parts)
+            e = e[w * i:w * i + w] if i + 1 < len(parts) else e[w * i:]
             many = isinstance(src, list)
-            ts.append(RemoteDMATransfer(dst_ids=[DstId(rid=rid, pnc=pid)], dma_engine_mask=sum(1 << k for k in e[w * i:w * i + w]),
+            ts.append(RemoteDMATransfer(dst_ids=[DstId(rid=rid, pnc=pid)], dma_engine_mask=sum(1 << k for k in e),
                                         remote_sem=sem, srcs=src if many else [src], dsts=[dst], alu_op=int(many)))
-            nsent[0] += w
+            nsent[0] += len(e)
         g.remote_dma_fused(ts, local_sem=T.sem.sent)
-
-    def codes(buf, c):
-        return buf[:, c:c + CH].bitcast(dt_u8)
 
     def send_codes(ds, c, buf, at, sem):
         fused([(d, codes(T.GQ, c + CH * i), codes(buf, at)) for i, d in enumerate(ds)], sem)
@@ -305,13 +366,27 @@ def rank_program(g, core, T, topo):
     dA, dB, dC = [[p, p + 1] for p in pairs]
     la, lb = CH * (r % 4), CH * (r % 2)
     need("g", hid)
-    fused([(d, [T.IXD[512 * k + 128 * (d // 2):512 * k + 128 * (d // 2) + 128, :] for k in range(4)], T.IXL[r])
-           for d in dA + dB + dC + [partner]], T.sem.arrX)
+    helpers = helpers_of(T, topo, r)
+    served = [d for _h, d in helpers]
+    out = topo.engines(core, T.cores[partner])
+
+    def windows(d):
+        return [T.IXD[1024 * k + 128 * d:1024 * k + 128 * d + 128, :] for k in range(8)]
+
+    def call(parts):
+        w = len(out) // 4
+        ts = [transfer(topo, T.cores[d], bits([e for k in qs for e in out[w * k:w * k + w]]), sem, src, dst)
+              for d, qs, sem, src, dst in parts]
+        nsent[0] += sum(w * len(p[1]) for p in parts)
+        g.remote_dma_fused(ts, local_sem=T.sem.sent)
+
+    fused([(d, windows(d), T.IXL[r]) for d in dA + dB + dC + [partner]], T.sem.arrX)
     need("g", hq1)
     send_codes(dA, 0, T.LAQ, la, T.sem.arrA)
+    send_scales(dA, 0, T.LAS, la, T.sem.arrA)
     need("g", hq2)
-    send_codes(dB, 128, T.LAQ, la, T.sem.arrA)
-    send_scales(dA + dB, 0, T.LAS, la, T.sem.arrA)
+    send_codes(dB, 128, T.LAQ, la, T.sem.arrD)
+    send_scales(dB, 128, T.LAS, la, T.sem.arrD)
     need("g", hq3)
     send_codes(dC, 256, T.LBQ, lb, T.sem.arrB)
     send_scales(dC, 256, T.LBS, lb, T.sem.arrB)
@@ -322,31 +397,44 @@ def rank_program(g, core, T, topo):
     def product(bank, o, q, sc):
         return te.matmul_mx(bank, T.WQ[:, 128 * o:128 * o + 128], T.WS[:, 128 * o:128 * o + 128], q, sc, True, True)
 
-    def take(src, o, inp, h):
-        out = T.Y[:, (2 * src + o) * CH:(2 * src + o) * CH + CH]
-        inc(h, v.tensor_copy(out, inp) if o == 0 else s.activation(out, inp, Copy))
-
     def finish(srcs, c0, banks, q, sc, n):
         hp = [one(product(buf[:, at:at + n], o, q, sc)) for o, (buf, at) in enumerate(banks)]
+        lo, hi = min(srcs), max(srcs) + 1
         hs = [ev(), ev()]
-        need("v", hp[0])
-        need("s", hp[1])
-        for i, src in enumerate(srcs):
-            for o, (buf, at) in enumerate(banks):
-                take(src, o, buf[:, at + c0 + CH * i:at + c0 + CH * i + CH], hs[o])
+        parts = [(lo, hi, 0)] if srcs[0] == lo else [(k, k + 1, CH * i) for i, k in enumerate(srcs)]
+        for o, (buf, at) in enumerate(banks):
+            need("vs"[o], hp[o])
+            for a, b, c in parts:
+                dst, inp = T.Y[:, a:b, o, :], buf[:, at + c0 + c:at + c0 + c + CH * (b - a)]
+                inc(hs[o], v.tensor_copy(dst, inp) if o == 0 else s.activation(dst, inp, Copy))
         need("y", *hs)
-        lo, hi = 128 * srcs[0], 128 * srcs[-1] + 128
-        one(sy.dma_start(T.y[:, lo:hi], T.Y[:, lo:hi]), 16)
+        one(sy.dma_start(T.y[:, 128 * lo:128 * hi], T.Y[:, lo:hi]), 16)
+        return hs
+
+    others = [(a, b) for a, b in ((0, r), (r + 1, N)) if a < b]
+    hnb = ev()
+    sy.wait_ge(T.sem.arrX, 8)
+    need("y", hnz)
+    for a, b in others:
+        inc(hnb, sy.dma_start(T.NB[a:b], T.IXL[a:b, :, 0]), 16)
+    need("y", hif)
+    one(sy.dma_start(T.ix[r:r + 1, :], T.IF[4 * r:4 * r + 4, :]), 16)
+
+    def far(n, sem, ds, banks):
+        te.wait_ge(sem, n)
+        c = CH * (ds[0] % 4)
+        finish(ds, 0, banks, T.LAQ[:, c:c + 128], T.LAS[:, c:c + 128], 128)
 
     need("t", hwq, hq5)
-    finish([r], CH, ((T.VB0, 0), (T.SB0, 0)), T.GQ[:, 512:640], T.GS[:, 512:640], 128)
-    sy.wait_ge(T.sem.arrX, 7)
-    for a, b in ((0, r), (r + 1, N)):
-        if a < b:
-            one(sy.dma_start(T.ix[a:b, :], T.IXL[a:b, lb:lb + CH, 0]), 16)
-    te.wait_ge(T.sem.arrA, 24)
-    oth = 4 * (1 - r // 4)
-    finish(range(oth, oth + 4), 0, ((T.SC, 0), (T.SC, 512)), T.LAQ[:], T.LAS[:], 256)
+    hown = finish([r], CH, ((T.VB0, 0), (T.SB0, 0)), T.GQ[:, 512:640], T.GS[:, 512:640], 128)
+    far(16, T.sem.arrA, dA, ((T.SC, 0), (T.SC, 512)))
+    need("v", hnb)
+    h = one(v.tensor_scalar(T.NF[0:N], T.NB[0:N, :, 0:16], 256.0, None, add))
+    need("y", h)
+    for a, b in others:
+        one(sy.dma_start(T.ix[a:b, :], T.NF[a:b]), 16)
+    need("t", *hown)
+    far(16, T.sem.arrD, dB, ((T.VB0, 0), (T.SB0, 0)))
     te.wait_ge(T.sem.arrB, 16)
     finish(dC, 0, ((T.SC, 1024), (T.SC, 1536)), T.LBQ[:, 0:128], T.LBS[:, 0:128], 128)
     te.wait_ge(T.sem.arrC, 16)

@@ -25,15 +25,15 @@ SCRATCH = {
     "QS": ("sbuf", [128, 4 * QW], "bfloat16"),
     "PK": ("sbuf", [128, 2], "float32"), "KK": ("sbuf", [128, 2], "float32"),
     "OF": ("sbuf", [128, 8], "uint16"),
-    "SW": ("sbuf", [128, 1024], "bfloat16"), "TT": ("sbuf", [128, 1024], "bfloat16"),
-    "Z": ("sbuf", [128, 128], "bfloat16"), "HA": ("sbuf", [128, 64], "bfloat16"), "HB": ("sbuf", [128, 32], "bfloat16"),
+    "SW": ("sbuf", [128, 1024], "bfloat16"),
+    "R": ("sbuf", [128, 256], "bfloat16"), "TT": ("sbuf", [128, 256], "bfloat16"),
+    "M8": ("sbuf", [128, 64], "bfloat16"), "SN": ("sbuf", [128, 256], "bfloat16"), "HB": ("sbuf", [128, 32], "bfloat16"),
     "OT": ("sbuf", [128, 32], "uint16"),
     "PL": ("sbuf", [128, 2048], "bfloat16"),
-    "G": ("sbuf", [128, 2304], "bfloat16"),
-    "GQ": ("sbuf", [128, 768], MX4), "GS": ("sbuf", [128, 768], "uint8"),
+    "G": ("sbuf", [128, 2048], "bfloat16"),
+    "GQ": ("sbuf", [128, 640], MX4), "GS": ("sbuf", [128, 640], "uint8"),
     "LAQ": ("sbuf", [128, 256], MX4), "LAS": ("sbuf", [128, 256], "uint8"),
     "LBQ": ("sbuf", [128, 192], MX4), "LBS": ("sbuf", [128, 192], "uint8"),
-    "HQ": ("sbuf", [128, CH], MX4), "HS": ("sbuf", [128, CH], "uint8"),
     "IV": ("sbuf", [128, 32], "bfloat16"), "IF": ("sbuf", [128, 16], "float32"),
     "NB": ("sbuf", [128, 4, 32], "bfloat16"), "NF": ("sbuf", [128, 4, 16], "float32"),
     "IXD": ("dram", [8192, 1], "bfloat16"), "IXL": ("dram", [8, 128, 1], "bfloat16"),
@@ -43,34 +43,8 @@ SCRATCH = {
     "SC": ("psum", [128, 2048], "float32"),
 }
 NEV = 140
-SEMAPHORES = ["arrA", "arrB", "arrC", "arrD", "arrH", "arrX", "sent"] + ["e%d" % i for i in range(NEV)]
+SEMAPHORES = ["arrA", "arrB", "arrC", "arrD", "arrX", "sent"] + ["e%d" % i for i in range(NEV)]
 MAGIC = 2304.0
-
-
-HELPERS = 0
-
-
-def transfer(topo, to, mask, sem, src, dst):
-    rid, pid, _se = topo.addr(to)
-    many = isinstance(src, list)
-    return RemoteDMATransfer(dst_ids=[DstId(rid=rid, pnc=pid)], dma_engine_mask=mask, remote_sem=sem,
-                             srcs=src if many else [src], dsts=[dst], alu_op=int(many))
-
-
-def helpers_of(T, topo, r):
-    core = T.cores[r]
-    free = [c for c in topo.cores_of(core) if c != core and topo.die(c) == topo.die(core)]
-    out = []
-    for k, near in ((6, False), (4, True)):
-        d = [j for j in (r ^ k, r ^ k ^ 1) if topo.same_plane(topo.chip(core), topo.chip(T.cores[j])) == near][0]
-        h = [c for c in free if topo.may_write(c, T.cores[d])][0]
-        free.remove(h)
-        out.append((h, d))
-    return out[:HELPERS]
-
-
-def bits(engines):
-    return sum(1 << e for e in engines)
 
 
 def codes(buf, c):
@@ -84,19 +58,8 @@ def scales(buf, c):
 def rank_program(g, core, T, topo):
     r = T.rank_of(core)
     if r is None:
-        for k in range(N):
-            for i, (helper, d) in enumerate(helpers_of(T, topo, k)):
-                if helper != core:
-                    continue
-                m, at, arr = topo.mask(core, T.cores[d]), CH * (k % 4), T.sem[("arrA", "arrD")[i]]
-                for got, n, sem, src, dst in ((T.sem.arrX, 8 // HELPERS, T.sem.arrX, T.IXL[k], T.IXL[k]),
-                                              (T.sem.arrA, 8, arr, codes(T.HQ, 0), codes(T.LAQ, at)),
-                                              (T.sem.arrB, 8, arr, scales(T.HS, 0), scales(T.LAS, at))):
-                    g.wait_ge(got, n)
-                    g.remote_dma_fused([transfer(topo, T.cores[d], m, sem, src, dst)], local_sem=T.sem.sent)
-                g.wait_ge(T.sem.sent, 24)
         return
-    add, sub, mult = AluOpType.add, AluOpType.subtract, AluOpType.mult
+    add, mult = AluOpType.add, AluOpType.mult
     ge, gt = AluOpType.is_ge, AluOpType.is_gt
     F = ActivationFunctionType
     Copy = F.Copy
@@ -147,6 +110,7 @@ def rank_program(g, core, T, topo):
         inc(hm, g.affine_select(T.MK[:, MW * b:MW * b + MW], T.ONE[:], [[1, MW]], AluOpType.not_equal, -1.0,
                                 -1 - 128 * b, -1))
     hsw = one(iota(T.SW[:], [[0, 1024]], 0))
+    hm8 = one(g.affine_select(T.M8[:], T.ONE[:, 0:64], [[0, 8], [1, 8]], gt, 0.0, 0, 0))
     need("v", hpi)
     hui = one(v.tensor_scalar(T.UI[:], T.PI[:], 3, None, AluOpType.bitwise_and))
     hgi = one(v.tensor_scalar(T.GI[:, 0:1], T.PI[:, 0:1], 112, None, AluOpType.bitwise_and))
@@ -164,7 +128,7 @@ def rank_program(g, core, T, topo):
     need("v", huo, hu)
     hur0 = one(v.tensor_copy(T.UR[:, 0:224], T.UB[:, 0:16].indirect(T.UO[:, 0:14])))
 
-    hq, hsc, hvb, hsb, hcol = [None] * 4, [None] * 4, [None] * 2, [None] * 2, [None] * 2
+    hq, hsc, hvb, hsb, hcol = [None] * 4, [None] * 4, [None] * 2, [None] * 2, [None] * 4
     huq = ev()
 
     def quant_x(a):
@@ -182,15 +146,16 @@ def rank_program(g, core, T, topo):
         return one(te.matmul_mx(T[bank % b][:, 0:256], T.UQ[:], T.US[:], T.XQ[:, 256 * b:256 * b + 256],
                                 T.XS[:, 256 * b:256 * b + 256], True, True))
 
-    hsg, hab, hcmp, htot, hpos, hxm = {}, {}, {}, {}, {}, {}
+    hsg, hab, hcmp, htot, hpos = {}, {}, {}, {}, {}
 
-    def keep(b, *hs):
-        need("s", hsc[2 * b], hsc[2 * b + 1], *hs)
-        hcol[b] = one(s.activation(T.SCS[:, 2 * b:2 * b + 2], T.SC[:, 1024 * b:1024 * b + 1024:512], Copy))
+    def keep(q, a, n, *hs):
+        need(q, *(hsc[a:a + n] + list(hs)))
+        out, inp = T.SCS[:, a:a + n], T.SC[:, 512 * a:512 * (a + n):512]
+        hcol[a:a + n] = [one(v.tensor_copy(out, inp) if q == "v" else s.activation(out, inp, Copy))] * n
 
     def signs(a):
         b = a // 2
-        need("s", hcol[b], hsb[b])
+        need("s", hcol[a], hsb[b])
         hsg[a] = one(s.activation(T.SG[:, 256 * a:256 * a + 256], T["SB%d" % b][:, 0:256], F.Sign,
                                   bias=T.SCS[:, a:a + 1], scale=-1.0, accum_out=T.AC[:, a:a + 1]))
 
@@ -200,7 +165,7 @@ def rank_program(g, core, T, topo):
 
     def compare(a):
         b = 1 - a // 2
-        need("v", hvb[b], hsc[a] if b == 0 else hcol[0])
+        need("v", hvb[b], hsc[a] if b == 0 else hcol[a])
         own = T.SC[:, 512 * a:512 * a + 1] if b == 0 else T.SCS[:, a:a + 1]
         hcmp[a] = one(v.tensor_scalar(T.C[:, 256 * a:256 * a + 256], T["VB%d" % b][:, 0:256], own, -2.0,
                                       gt if b else ge, mult))
@@ -217,15 +182,12 @@ def rank_program(g, core, T, topo):
         hpos[a] = one(v.tensor_tensor_scan(T.QS[:, QW * a:QW * a + 259], T.AB[:, AW * a + 127:AW * a + 386],
                                            T.MK[:, m:m + 259], T.AC[:, a:a + 1], add, mult))
 
-    def pos(a):
-        return T.QS[:, QW * a + 256:QW * a + 257]
-
     hof = [ev(), ev()]
 
     def offset(a):
         need("v", hpos[a])
-        inc(hof[a // 2], v.tensor_scalar(T.OF[:, 2 * a:2 * a + 2], T.KK[:], T.QS[:, QW * a + 258:QW * a + 259], pos(a),
-                                         add, add))
+        c = QW * a + 256
+        inc(hof[a // 2], v.tensor_scalar(T.OF[:, 2 * a:2 * a + 2], T.KK[:], T.QS[:, c + 2:c + 3], T.QS[:, c:c + 1], add, add))
 
     def scatter(b, *hs):
         need("v", hof[b], hsw, hj, *hs)
@@ -236,8 +198,8 @@ def rank_program(g, core, T, topo):
     inc(huq, v.quantize_mx(T.UQ[:], T.US[:], T.UR[:]))
     score_col(0)
     quant_x(1)
-    score_col(1)
     hsb[0] = score_row("SB%d", 0)
+    score_col(1)
     hvb[0] = score_row("VB%d", 0)
     quant_x(2)
     score_col(2)
@@ -245,44 +207,23 @@ def rank_program(g, core, T, topo):
     score_col(3)
     hvb[1] = score_row("VB%d", 1)
     hsb[1] = score_row("SB%d", 1)
+    keep("v", 1, 1)
     compare(2); compare(3)
     need("s", hm)
     hmk = one(s.activation(T.MK[:, 256:2 * MW:MW], T.MK[:, 256:2 * MW:MW], Copy, scale=0.5))
-    keep(0); signs(0); signs(1); sizes(0); keep(1, hcmp[2], hcmp[3]); sizes(1)
+    keep("s", 0, 1); signs(0); signs(1); sizes(0); keep("s", 2, 2, hcmp[2], hcmp[3]); sizes(1)
     signs(2); signs(3); sizes(2); sizes(3)
     compare(0); compare(1); total(0); total(1); late(0); late(1); offset(0); total(2); offset(1); total(3)
     h01 = scatter(0)
     late(2); late(3); offset(2); offset(3)
+    hwin = scatter(1, h01)
 
-    h = scatter(1, h01)
-    need("v", h)
-    hsc2 = h
-    own = r // 4
-    oth = 1 - own
-    htt, hz, hzd = {}, {}, {}
-
-    def turn(b):
-        htt[b] = one(v.transpose(T.TT[:, 512 * b:512 * b + 512], T.SW[:, 512 * b:512 * b + 512]))
-
-    def exchange(b, qs):
-        need("v", htt[b])
-        c = 512 * b
-        hz[b] = one(v.tensor_tensor(T.Z[:, 64 * b:64 * b + 16], T.TT[:, c:c + 512:32], T.TT[:, c + 16:c + 512:32], add))
-        hzd[b] = ev()
-        src = 64 * b
-        for k in (1, 2, 3):
-            m, dst = 32 * k, 64 * b + 16 * k
-            for qn, lo, hi, at in ((qs[0], 0, 128 - m, m), (qs[1], 128 - m, 128, 0)):
-                need(qn, hz[b])
-                inc(hzd[b], Q[qn].dma_start(T.Z[lo:hi, dst:dst + 16], T.Z[at:at + hi - lo, src:src + 16]), 16)
-
-    turn(oth)
-    exchange(oth, "ys")
-    need("y", hsc2)
+    hr = ev()
+    need("y", hwin)
+    need("s", hwin)
+    for k in range(4):
+        inc(hr, (s if k % 2 else sy).dma_start(T.R[32 * k:32 * k + 32, :], T.SW[0:128:16, :]), 16)
     hid = one(sy.dma_start(T.IXD[:, 0], T.SW[0:128:16, :]), 16)
-    turn(own)
-    exchange(own, "yy")
-
 
     hpl = [None] * 4
 
@@ -293,26 +234,24 @@ def rank_program(g, core, T, topo):
 
     plane("s", 3); plane("s", 2)
     plane("v", 0); plane("v", 1)
-    hot = {}
+    need("v", hw)
+    hwq = one(v.quantize_mx(T.WQ[:], T.WS[:], T.WB[:]))
+    need("v", hr)
+    htt = one(v.transpose(T.TT[:], T.R[:]))
+    hsn, hot = {}, {}
 
-    def whole(b):
-        need("v", hzd[b])
-        h = one(v.tensor_tensor(T.HA[:, 32 * b:32 * b + 32], T.Z[:, 64 * b:64 * b + 32], T.Z[:, 64 * b + 32:64 * b + 64], add))
-        yield
-        need("v", h)
-        h = one(v.tensor_tensor(T.HB[:, 16 * b:16 * b + 16], T.HA[:, 32 * b:32 * b + 16], T.HA[:, 32 * b + 16:32 * b + 32], add))
-        yield
-        need("v", h)
-        hot[b] = one(v.tensor_scalar(T.OT[:, 16 * b:16 * b + 16], T.HB[:, 16 * b:16 * b + 16], 256.0, None, add))
-        yield
+    def sums(j):
+        need("v", htt, hm8)
+        hsn[j] = one(v.tensor_tensor_scan(T.SN[:, 64 * j:64 * j + 64], T.M8[:], T.TT[:, j:256:4], 0.0, mult, add))
 
-    list(whole(oth))
-    later = whole(own)
+    def listed(j):
+        need("v", hsn[j])
+        hot[j] = one(v.tensor_scalar(T.OT[:, 8 * j:8 * j + 8], T.SN[:, 64 * j + 7:64 * j + 64:8], 256.0, None, add))
 
     def gather(q, h, run, n, slot, es):
         for e in es:
-            need(q, hot[run // 4], hpl[e])
-            out = T.G[:, 256 * (slot + 1) + e:256 * (slot + 1 + n):4]
+            need(q, hot[run // 2], hpl[e])
+            out = T.G[:, 256 * slot + e:256 * (slot + n):4]
             win = T.PL[:, 512 * e:512 * e + 512].indirect(T.OT[:, 4 * run:4 * (run + n)])
             inc(h, v.tensor_copy(out, win) if q == "v" else s.activation(out, win, Copy))
         return h
@@ -321,92 +260,69 @@ def rank_program(g, core, T, topo):
         return gather("v", ev(), run, n, slot, range(nv)), gather("s", ev(), run, n, slot, range(nv, 4))
 
     def quant(slot, c, hs):
-        need("v", *[h for h in hs if h[1]])
-        return one(v.quantize_mx(T.GQ[:, c:c + 128], T.GS[:, c:c + 128], T.G[:, 256 * slot + 256:256 * slot + 768]))
+        need("v", *hs)
+        return one(v.quantize_mx(T.GQ[:, c:c + 128], T.GS[:, c:c + 128], T.G[:, 256 * slot:256 * slot + 512]))
 
-    pairs = [2 * ((r // 2) ^ k) for k in (3, 2, 1)]
+    ja, jb, jc, jd = [(r // 2) ^ k for k in (3, 2, 1, 0)]
     partner = r ^ 1
-    hA = stage(pairs[0], 2, 0, 2)
-    next(later)
+    sums(ja); sums(jb); listed(ja); listed(jb)
+    hA = stage(2 * ja, 2, 0, 2)
+    sums(jc)
     hq1 = quant(0, 0, hA)
-    next(later)
-    hB = stage(pairs[1], 2, 2, 1)
-    next(later)
+    listed(jc)
+    hB = stage(2 * jb, 2, 2, 1)
+    hC = gather("v", ev(), 2 * jc, 2, 4, (0,)), gather("s", ev(), 2 * jc, 2, 4, (2, 3))
+    sums(jd)
     hq2 = quant(2, 128, hB)
-    hq3 = quant(4, 256, stage(pairs[2], 2, 4, 2))
-    hq4 = quant(5, 384, stage(partner, 1, 6, 0))
-    need("v", hw)
-    hwq = one(v.quantize_mx(T.WQ[:], T.WS[:], T.WB[:]))
+    listed(jd)
+    gather("v", hC[0], 2 * jc, 2, 4, (1,))
+    hD = gather("v", ev(), partner, 1, 6, (0,)), gather("s", ev(), partner, 1, 6, (2, 3))
+    hq3 = quant(4, 256, hC)
+    gather("v", hD[0], partner, 1, 6, (1,))
+    hq4 = quant(5, 384, hD)
     hq5 = quant(6, 512, stage(r, 1, 7, 1))
-    hiv = one(v.transpose(T.IV[:], T.HB[:]))
-    need("v", hiv)
+    h = one(v.tensor_copy(T.HB[:], T.SN[:, 7:256:8]))
+    need("v", h)
+    h = one(v.transpose(T.IV[:], T.HB[:]))
+    need("v", h)
     hif = one(v.tensor_scalar(T.IF[:], T.IV[:, 0:16], 256.0, None, add))
 
     nsent = [0]
 
     def fused(parts, sem):
         ts = []
-        for i, (d, src, dst) in enumerate(parts):
+        for i, (d, srcs, dst) in enumerate(parts):
             rid, pid, _se = topo.addr(T.cores[d])
             e = topo.engines(core, T.cores[d])
             w = len(e) // len(parts)
             e = e[w * i:w * i + w] if i + 1 < len(parts) else e[w * i:]
-            many = isinstance(src, list)
             ts.append(RemoteDMATransfer(dst_ids=[DstId(rid=rid, pnc=pid)], dma_engine_mask=sum(1 << k for k in e),
-                                        remote_sem=sem, srcs=src if many else [src], dsts=[dst], alu_op=int(many)))
+                                        remote_sem=sem, srcs=srcs, dsts=[dst], alu_op=int(len(srcs) > 1)))
             nsent[0] += len(e)
         g.remote_dma_fused(ts, local_sem=T.sem.sent)
 
-    def send_codes(ds, c, buf, at, sem):
-        fused([(d, codes(T.GQ, c + CH * i), codes(buf, at)) for i, d in enumerate(ds)], sem)
+    def send(h, ds, c, bufq, bufs, at, sem):
+        need("g", h)
+        fused([(d, [codes(T.GQ, c + CH * i)], codes(bufq, at)) for i, d in enumerate(ds)], sem)
+        fused([(d, [scales(T.GS, c + CH * i)], scales(bufs, at)) for i, d in enumerate(ds)], sem)
 
-    def send_scales(ds, c, buf, at, sem):
-        fused([(d, T.GS[:, c + CH * i:c + CH * i + CH], buf[:, at:at + CH]) for i, d in enumerate(ds)], sem)
-
-    dA, dB, dC = [[p, p + 1] for p in pairs]
-    la, lb = CH * (r % 4), CH * (r % 2)
+    dA, dB, dC = [[2 * j, 2 * j + 1] for j in (ja, jb, jc)]
     need("g", hid)
-    helpers = helpers_of(T, topo, r)
-    served = [d for _h, d in helpers]
-    out = topo.engines(core, T.cores[partner])
+    fused([(d, [T.IXD[1024 * k + 128 * d:1024 * k + 128 * d + 128, :] for k in range(8)], T.IXL[r])
+           for d in dA + dB + dC + [partner]], T.sem.arrX)
+    send(hq1, dA, 0, T.LAQ, T.LAS, CH * (r % 4), T.sem.arrA)
+    send(hq2, dB, 128, T.LAQ, T.LAS, CH * (r % 4), T.sem.arrB)
+    send(hq3, dC, 256, T.LBQ, T.LBS, CH * (r % 2), T.sem.arrC)
+    send(hq4, [partner], 448, T.LBQ, T.LBS, 128, T.sem.arrD)
 
-    def windows(d):
-        return [T.IXD[1024 * k + 128 * d:1024 * k + 128 * d + 128, :] for k in range(8)]
-
-    def call(parts):
-        w = len(out) // 4
-        ts = [transfer(topo, T.cores[d], bits([e for k in qs for e in out[w * k:w * k + w]]), sem, src, dst)
-              for d, qs, sem, src, dst in parts]
-        nsent[0] += sum(w * len(p[1]) for p in parts)
-        g.remote_dma_fused(ts, local_sem=T.sem.sent)
-
-    fused([(d, windows(d), T.IXL[r]) for d in dA + dB + dC + [partner]], T.sem.arrX)
-    need("g", hq1)
-    send_codes(dA, 0, T.LAQ, la, T.sem.arrA)
-    send_scales(dA, 0, T.LAS, la, T.sem.arrA)
-    need("g", hq2)
-    send_codes(dB, 128, T.LAQ, la, T.sem.arrD)
-    send_scales(dB, 128, T.LAS, la, T.sem.arrD)
-    need("g", hq3)
-    send_codes(dC, 256, T.LBQ, lb, T.sem.arrB)
-    send_scales(dC, 256, T.LBS, lb, T.sem.arrB)
-    need("g", hq4)
-    send_codes([partner], 448, T.LBQ, 128, T.sem.arrC)
-    send_scales([partner], 448, T.LBS, 128, T.sem.arrC)
-
-    def product(bank, o, q, sc):
-        return te.matmul_mx(bank, T.WQ[:, 128 * o:128 * o + 128], T.WS[:, 128 * o:128 * o + 128], q, sc, True, True)
-
-    def finish(srcs, c0, banks, q, sc, n):
-        hp = [one(product(buf[:, at:at + n], o, q, sc)) for o, (buf, at) in enumerate(banks)]
-        lo, hi = min(srcs), max(srcs) + 1
-        hs = [ev(), ev()]
-        parts = [(lo, hi, 0)] if srcs[0] == lo else [(k, k + 1, CH * i) for i, k in enumerate(srcs)]
+    def finish(lo, hi, c0, banks, bufq, bufs, c):
+        hp = [one(te.matmul_mx(buf[:, at:at + 128], T.WQ[:, 128 * o:128 * o + 128], T.WS[:, 128 * o:128 * o + 128],
+                               bufq[:, c:c + 128], bufs[:, c:c + 128], True, True)) for o, (buf, at) in enumerate(banks)]
+        hs = []
         for o, (buf, at) in enumerate(banks):
             need("vs"[o], hp[o])
-            for a, b, c in parts:
-                dst, inp = T.Y[:, a:b, o, :], buf[:, at + c0 + c:at + c0 + c + CH * (b - a)]
-                inc(hs[o], v.tensor_copy(dst, inp) if o == 0 else s.activation(dst, inp, Copy))
+            dst, inp = T.Y[:, lo:hi, o, :], buf[:, at + c0:at + c0 + CH * (hi - lo)]
+            hs.append(one(v.tensor_copy(dst, inp) if o == 0 else s.activation(dst, inp, Copy)))
         need("y", *hs)
         one(sy.dma_start(T.y[:, 128 * lo:128 * hi], T.Y[:, lo:hi]), 16)
         return hs
@@ -420,25 +336,22 @@ def rank_program(g, core, T, topo):
     need("y", hif)
     one(sy.dma_start(T.ix[r:r + 1, :], T.IF[4 * r:4 * r + 4, :]), 16)
 
-    def far(n, sem, ds, banks):
-        te.wait_ge(sem, n)
-        c = CH * (ds[0] % 4)
-        finish(ds, 0, banks, T.LAQ[:, c:c + 128], T.LAS[:, c:c + 128], 128)
-
     need("t", hwq, hq5)
-    hown = finish([r], CH, ((T.VB0, 0), (T.SB0, 0)), T.GQ[:, 512:640], T.GS[:, 512:640], 128)
-    far(16, T.sem.arrA, dA, ((T.SC, 0), (T.SC, 512)))
+    hown = finish(r, r + 1, CH, ((T.VB0, 0), (T.SB0, 0)), T.GQ, T.GS, 512)
+    te.wait_ge(T.sem.arrA, 16)
+    finish(dA[0], dA[0] + 2, 0, ((T.SC, 0), (T.SC, 512)), T.LAQ, T.LAS, CH * (dA[0] % 4))
     need("v", hnb)
     h = one(v.tensor_scalar(T.NF[0:N], T.NB[0:N, :, 0:16], 256.0, None, add))
     need("y", h)
     for a, b in others:
         one(sy.dma_start(T.ix[a:b, :], T.NF[a:b]), 16)
     need("t", *hown)
-    far(16, T.sem.arrD, dB, ((T.VB0, 0), (T.SB0, 0)))
     te.wait_ge(T.sem.arrB, 16)
-    finish(dC, 0, ((T.SC, 1024), (T.SC, 1536)), T.LBQ[:, 0:128], T.LBS[:, 0:128], 128)
+    finish(dB[0], dB[0] + 2, 0, ((T.VB0, 0), (T.SB0, 0)), T.LAQ, T.LAS, CH * (dB[0] % 4))
     te.wait_ge(T.sem.arrC, 16)
-    finish([partner], CH, ((T.VB1, 0), (T.SB1, 0)), T.LBQ[:, 64:192], T.LBS[:, 64:192], 128)
+    finish(dC[0], dC[0] + 2, 0, ((T.SC, 1024), (T.SC, 1536)), T.LBQ, T.LBS, 0)
+    te.wait_ge(T.sem.arrD, 16)
+    finish(partner, partner + 1, CH, ((T.VB1, 0), (T.SB1, 0)), T.LBQ, T.LBS, 64)
 
     g.wait_ge(T.sem.sent, nsent[0])
     for h in events:

@@ -3,7 +3,6 @@ from concourse.mybir import dt, AluOpType, ActivationFunctionType
 
 N, TC, O, CH = 8, 512, 2, 64
 MX4 = "float8_e4m3fn_x4"
-AW, MW, QW = 392, 260, 264
 SCRATCH = {
     "UB": ("sbuf", [128, 16], "bfloat16"),
     "UR": ("sbuf", [128, 512], "bfloat16"),
@@ -14,29 +13,30 @@ SCRATCH = {
     "WQ": ("sbuf", [128, 256], MX4), "WS": ("sbuf", [128, 256], "uint8"),
     "PI": ("sbuf", [128, 32], "int32"),
     "UI": ("sbuf", [128, 32], "int32"), "UO": ("sbuf", [128, 32], "uint16"),
-    "GI": ("sbuf", [128, 8], "int32"), "GF": ("sbuf", [128, 8], "float32"),
-    "JF": ("sbuf", [128, 128], "float32"), "J": ("sbuf", [128, 128], "bfloat16"),
-    "ONE": ("sbuf", [128, MW], "bfloat16"), "MK": ("sbuf", [128, 2 * MW], "bfloat16"),
-    "SCS": ("sbuf", [128, 4], "float32"),
-    "C": ("sbuf", [128, 1024], "bfloat16"),
-    "SG": ("sbuf", [128, 1024], "bfloat16"),
-    "AB": ("sbuf", [128, 4 * AW], "bfloat16"),
+    "PF": ("sbuf", [128, 4], "float32"), "FB": ("sbuf", [128, 8], "bfloat16"),
+    "EB": ("sbuf", [128, 8], "float32"),
+    "JF": ("sbuf", [128, 64], "float32"), "J": ("sbuf", [128, 64], "bfloat16"),
+    "MK": ("sbuf", [128, 3, 392], "bfloat16"),
+    "SCS": ("sbuf", [128, 2], "float32"),
+    "SG": ("sbuf", [128, 4, 256], "bfloat16"),
+    "AB": ("sbuf", [128, 2, 264], "bfloat16"),
     "AC": ("sbuf", [128, 4], "float32"),
-    "QS": ("sbuf", [128, 4 * QW], "bfloat16"),
-    "PK": ("sbuf", [128, 2], "float32"), "KK": ("sbuf", [128, 2], "float32"),
+    "C": ("sbuf", [128, 6, 256], "bfloat16"),
+    "QS": ("sbuf", [128, 8, 264], "bfloat16"),
+    "PK": ("sbuf", [128, 2], "bfloat16"),
     "OF": ("sbuf", [128, 8], "uint16"),
-    "SW": ("sbuf", [128, 1024], "bfloat16"),
-    "R": ("sbuf", [128, 256], "bfloat16"), "TT": ("sbuf", [128, 256], "bfloat16"),
-    "M8": ("sbuf", [128, 64], "bfloat16"), "SN": ("sbuf", [128, 256], "bfloat16"), "HB": ("sbuf", [128, 32], "bfloat16"),
-    "OT": ("sbuf", [128, 32], "uint16"),
-    "PL": ("sbuf", [128, 2048], "bfloat16"),
+    "SW": ("sbuf", [128, 512], "bfloat16"),
+    "TT": ("sbuf", [128, 4, 16, 8], "bfloat16"),
+    "P": ("sbuf", [128, 4, 32], "bfloat16"), "H": ("sbuf", [128, 4, 32], "bfloat16"),
+    "K": ("sbuf", [128, 4, 32], "bfloat16"), "ZT": ("sbuf", [128, 4, 32], "bfloat16"),
+    "OT": ("sbuf", [128, 128], "uint16"),
     "G": ("sbuf", [128, 2048], "bfloat16"),
     "GQ": ("sbuf", [128, 640], MX4), "GS": ("sbuf", [128, 640], "uint8"),
     "LAQ": ("sbuf", [128, 256], MX4), "LAS": ("sbuf", [128, 256], "uint8"),
     "LBQ": ("sbuf", [128, 192], MX4), "LBS": ("sbuf", [128, 192], "uint8"),
-    "IV": ("sbuf", [128, 32], "bfloat16"), "IF": ("sbuf", [128, 16], "float32"),
-    "NB": ("sbuf", [128, 4, 32], "bfloat16"), "NF": ("sbuf", [128, 4, 16], "float32"),
-    "IXD": ("dram", [8192, 1], "bfloat16"), "IXL": ("dram", [8, 128, 1], "bfloat16"),
+    "IF": ("sbuf", [128, 4], "float32"),
+    "NF": ("sbuf", [128, 64], "float32"),
+    "IXD": ("dram", [4096, 1], "bfloat16"), "IXL": ("dram", [8, 128, 1], "bfloat16"),
     "Y": ("sbuf", [128, N, O, CH], "float32"),
     "VB0": ("psum", [128, 512], "float32"), "VB1": ("psum", [128, 512], "float32"),
     "SB0": ("psum", [128, 512], "float32"), "SB1": ("psum", [128, 512], "float32"),
@@ -44,7 +44,6 @@ SCRATCH = {
 }
 NEV = 140
 SEMAPHORES = ["arrA", "arrB", "arrC", "arrD", "arrX", "sent"] + ["e%d" % i for i in range(NEV)]
-MAGIC = 2304.0
 
 
 def codes(buf, c):
@@ -60,7 +59,7 @@ def rank_program(g, core, T, topo):
     if r is None:
         return
     add, mult = AluOpType.add, AluOpType.mult
-    ge, gt = AluOpType.is_ge, AluOpType.is_gt
+    ge, gt, ne = AluOpType.is_ge, AluOpType.is_gt, AluOpType.not_equal
     F = ActivationFunctionType
     Copy = F.Copy
     v, s, te, sy = g.vector, g.scalar, g.tensor, g.sync
@@ -98,37 +97,35 @@ def rank_program(g, core, T, topo):
         return g.iota(out, pattern, base, step, allow_small_or_imprecise_dtypes=True)
 
     hpi = one(g.iota(T.PI[:], [[0, 32]], 0, 1))
-    hone = one(v.memset(T.ONE[:], 1.0))
-    hkk = ev()
-    inc(hkk, v.memset(T.KK[:, 0:1], 256.0 - MAGIC))
-    inc(hkk, v.memset(T.KK[:, 1:2], 272.0 - MAGIC))
-    hjf = one(iota(T.JF[:], [[128, 4], [0, 2], [1, 16]], -256))
-    hpk = one(iota(T.PK[:], [[-256, 2]], 512, -2))
-    need("g", hone)
-    hm = ev()
-    for b in range(2):
-        inc(hm, g.affine_select(T.MK[:, MW * b:MW * b + MW], T.ONE[:], [[1, MW]], AluOpType.not_equal, -1.0,
-                                -1 - 128 * b, -1))
-    hsw = one(iota(T.SW[:], [[0, 1024]], 0))
-    hm8 = one(g.affine_select(T.M8[:], T.ONE[:, 0:64], [[0, 8], [1, 8]], gt, 0.0, 0, 0))
+    hpf = one(iota(T.PF[:], [[1664 - 2296, 2], [638 - 2296, 2]], 2296, 1))
+    hjf = one(iota(T.JF[:], [[128, 4], [1, 16]], -256 - 2304))
     need("v", hpi)
     hui = one(v.tensor_scalar(T.UI[:], T.PI[:], 3, None, AluOpType.bitwise_and))
-    hgi = one(v.tensor_scalar(T.GI[:, 0:1], T.PI[:, 0:1], 112, None, AluOpType.bitwise_and))
+    hone = one(v.memset(T.MK[:], 1.0))
+    need("g", hone)
+    hm = ev()
+    for k, (c, fill, step, base) in enumerate(((129, -1.0, -1, 0), (0, 0.0, -1, 0), (0, 0.0, 1, -127))):
+        inc(hm, g.affine_select(T.MK[:, k, c:c + 128], T.MK[:, k, c:c + 128], [[1, 128]], ne, fill, base, step))
+    hpk = one(iota(T.PK[:], [[-256, 2]], 0, -2))
+    hsw = one(iota(T.SW[:], [[0, 512]], 0))
+    hnz = one(iota(T.NF[0:N], [[0, 64]], 256))
     need("v", hui)
     huo = one(v.tensor_copy(T.UO[:], T.UI[:]))
-    need("v", hgi)
-    hgf = one(v.tensor_copy(T.GF[:, 0:1], T.GI[:, 0:1]))
-    inc(hkk, v.memset(T.AB[:, 384:4 * AW:AW], MAGIC + 256.0))
-    inc(hkk, v.memset(T.AB[:, 385:4 * AW:AW], -7.5))
-    hnz = one(v.memset(T.NB[0:N], 0.0))
-    need("s", hgf, hjf)
-    hj = one(s.activation(T.J[:], T.JF[:], F.Identity, bias=T.GF[:, 0:1]))
+    need("s", hpf)
+    hfb = one(s.activation(T.FB[:, 0:2], T.PF[:, 0:2], F.Identity, bias=0.5))
+    need("s", hfb)
+    heb = one(s.activation(T.EB[:, 0:1], T.FB[:, 1:2], F.Identity, bias=T.PF[:, 2:3], scale=-1.0))
+    need("y", hnz)
+    others = [(a, b) for a, b in ((0, r), (r + 1, N)) if a < b]
+    hfill = ev()
+    for a, b in others:
+        inc(hfill, sy.dma_start(T.ix[a:b, :], T.NF[a:b]), 16)
     need("s", huo, hu)
     hur1 = one(s.activation(T.UR[:, 224:512], T.UB[:, 0:16].indirect(T.UO[:, 14:32]), Copy))
     need("v", huo, hu)
     hur0 = one(v.tensor_copy(T.UR[:, 0:224], T.UB[:, 0:16].indirect(T.UO[:, 0:14])))
 
-    hq, hsc, hvb, hsb, hcol = [None] * 4, [None] * 4, [None] * 2, [None] * 2, [None] * 4
+    hq, hsc, hvb, hsb = [None] * 4, [None] * 4, [None] * 2, [None] * 2
     huq = ev()
 
     def quant_x(a):
@@ -146,146 +143,120 @@ def rank_program(g, core, T, topo):
         return one(te.matmul_mx(T[bank % b][:, 0:256], T.UQ[:], T.US[:], T.XQ[:, 256 * b:256 * b + 256],
                                 T.XS[:, 256 * b:256 * b + 256], True, True))
 
-    hsg, hab, hcmp, htot, hpos = {}, {}, {}, {}, {}
-
-    def keep(q, a, n, *hs):
-        need(q, *(hsc[a:a + n] + list(hs)))
-        out, inp = T.SCS[:, a:a + n], T.SC[:, 512 * a:512 * (a + n):512]
-        hcol[a:a + n] = [one(v.tensor_copy(out, inp) if q == "v" else s.activation(out, inp, Copy))] * n
-
-    def signs(a):
-        b = a // 2
-        need("s", hcol[a], hsb[b])
-        hsg[a] = one(s.activation(T.SG[:, 256 * a:256 * a + 256], T["SB%d" % b][:, 0:256], F.Sign,
-                                  bias=T.SCS[:, a:a + 1], scale=-1.0, accum_out=T.AC[:, a:a + 1]))
-
-    def sizes(a):
-        need("s", hsg[a])
-        hab[a] = one(s.activation(T.AB[:, AW * a + 128:AW * a + 384], T.SG[:, 256 * a:256 * a + 256], F.Abs))
-
-    def compare(a):
-        b = 1 - a // 2
-        need("v", hvb[b], hsc[a] if b == 0 else hcol[a])
-        own = T.SC[:, 512 * a:512 * a + 1] if b == 0 else T.SCS[:, a:a + 1]
-        hcmp[a] = one(v.tensor_scalar(T.C[:, 256 * a:256 * a + 256], T["VB%d" % b][:, 0:256], own, -2.0,
-                                      gt if b else ge, mult))
-
-    def total(a):
-        need("v", hcmp[a], hpk)
-        c = 256 * a
-        htot[a] = one(v.tensor_tensor_scan(T.AB[:, AW * a:AW * a + 128], T.C[:, c:c + 128], T.C[:, c + 128:c + 256],
-                                           T.PK[:, a % 2:a % 2 + 1], add, add))
-
-    def late(a):
-        need("v", htot[a], hab[a], hmk, hkk)
-        m = MW * (a % 2)
-        hpos[a] = one(v.tensor_tensor_scan(T.QS[:, QW * a:QW * a + 259], T.AB[:, AW * a + 127:AW * a + 386],
-                                           T.MK[:, m:m + 259], T.AC[:, a:a + 1], add, mult))
-
-    hof = [ev(), ev()]
-
-    def offset(a):
-        need("v", hpos[a])
-        c = QW * a + 256
-        inc(hof[a // 2], v.tensor_scalar(T.OF[:, 2 * a:2 * a + 2], T.KK[:], T.QS[:, c + 2:c + 3], T.QS[:, c:c + 1], add, add))
-
-    def scatter(b, *hs):
-        need("v", hof[b], hsw, hj, *hs)
-        return one(v.tensor_copy(T.SW[:, 0:1024].indirect(T.OF[:, 4 * b:4 * b + 4]), T.J[:, 64 * b:64 * b + 64]))
-
     quant_x(0)
     need("v", hur0, hur1)
     inc(huq, v.quantize_mx(T.UQ[:], T.US[:], T.UR[:]))
     score_col(0)
     quant_x(1)
-    hsb[0] = score_row("SB%d", 0)
     score_col(1)
     hvb[0] = score_row("VB%d", 0)
     quant_x(2)
     score_col(2)
+    hsb[0] = score_row("SB%d", 0)
     quant_x(3)
     score_col(3)
     hvb[1] = score_row("VB%d", 1)
     hsb[1] = score_row("SB%d", 1)
-    keep("v", 1, 1)
-    compare(2); compare(3)
-    need("s", hm)
-    hmk = one(s.activation(T.MK[:, 256:2 * MW:MW], T.MK[:, 256:2 * MW:MW], Copy, scale=0.5))
-    keep("s", 0, 1); signs(0); signs(1); sizes(0); keep("s", 2, 2, hcmp[2], hcmp[3]); sizes(1)
-    signs(2); signs(3); sizes(2); sizes(3)
-    compare(0); compare(1); total(0); total(1); late(0); late(1); offset(0); total(2); offset(1); total(3)
-    h01 = scatter(0)
-    late(2); late(3); offset(2); offset(3)
-    hwin = scatter(1, h01)
 
-    hr = ev()
+    need("s", hsc[0], hsc[1])
+    hcol = one(s.activation(T.SCS[:], T.SC[:, 0:1024:512], Copy))
+    need("s", hjf)
+    hj = one(s.activation(T.J[:], T.JF[:], F.Identity, bias=T.FB[:, 0:1]))
+
+    def signs(a, b, **kw):
+        need("s", hcol, hsb[b])
+        return one(s.activation(T.SG[:, 2 * b + a, :], T["SB%d" % b][:, 0:256], F.Sign, bias=T.SCS[:, a:a + 1], scale=-1.0, **kw))
+
+    hsg = [signs(a, 0, accum_out=T.AC[:, a:a + 1]) for a in range(2)]
+    hab = []
+    for a in range(2):
+        need("s", hsg[a])
+        hab.append(one(s.activation(T.AB[:, a, 1:257], T.SG[:, a, :], F.Abs)))
+    hup = [signs(a, 1) for a in range(2)]
+    hct = []
+    for a in range(2):
+        need("s", hup[a])
+        hct.append(one(s.activation(T.SG[:, 2 + a, :], T.SG[:, 2 + a, :], F.Relu, scale=-1.0, accum_out=T.AC[:, 2 + a:3 + a])))
+
+    def flags(k, a, b, view, op):
+        need("v", hvb[b], hsc[a])
+        return one(v.tensor_scalar(T.C[:, k, 0:view.shape[1]], view, T.SC[:, 512 * a:512 * a + 1], None, op))
+
+    def scan(k, n, d0, d1, first, op, *hs):
+        need("v", *hs)
+        return one(v.tensor_tensor_scan(T.QS[:, k, 264 - n:264], d0, d1, first, add, op))
+
+    hf = [flags(0, 2, 0, T.VB0[:, 0:256], ge), flags(1, 3, 0, T.VB0[:, 0:256], ge),
+          flags(2, 2, 1, T.VB1[:, 0:256], gt), flags(3, 3, 1, T.VB1[:, 255::-1], ge),
+          flags(4, 2, 1, T.VB1[:, 127::-1], ge), flags(5, 3, 1, T.VB1[:, 128:256], gt)]
+    need("v", *hsg)
+    hac = one(v.tensor_copy(T.AB[:, :, 0], T.AC[:, 0:2]))
+    hs = [scan(k, 128, T.C[:, k, 0:128], T.C[:, k, 128:256], 0.0, add, hf[k]) for k in range(2)]
+    hs += [scan(k, n, T.C[:, k, 0:n], T.MK[:, m, 0:n], 0.0, mult, hf[k], hm)
+           for k, n, m in ((2, 256, 1), (3, 256, 2), (4, 128, 2), (5, 128, 1))]
+    hs += [scan(6 + a, 257, T.AB[:, a, 0:257], T.MK[:, 0, 128 - 128 * a:385 - 128 * a], T.PK[:, a:a + 1], mult, hac, hab[a], hpk)
+           for a in range(2)]
+    hof = ev()
+    for a in range(2):
+        need("v", hs[a], hs[2 + a], hs[4 + a])
+        inc(hof, v.tensor_scalar(T.OF[:, 2 + a:3 + a], T.QS[:, a, 263:264], T.QS[:, 2 + a, 263:264], T.QS[:, 4 + a, 263:264], add, add))
+    for a in range(2):
+        need("v", hs[6 + a], hct[a])
+        inc(hof, v.tensor_scalar(T.OF[:, a:a + 1], T.QS[:, 6 + a, 263:264], 0.5, T.AC[:, 2 + a:3 + a], mult, add))
+    need("v", hof, hsw, hj)
+    hwin = one(v.tensor_copy(T.SW[:, 0:512].indirect(T.OF[:, 0:4]), T.J[:]))
+
     need("y", hwin)
-    need("s", hwin)
-    for k in range(4):
-        inc(hr, (s if k % 2 else sy).dma_start(T.R[32 * k:32 * k + 32, :], T.SW[0:128:16, :]), 16)
     hid = one(sy.dma_start(T.IXD[:, 0], T.SW[0:128:16, :]), 16)
+    need("v", hwin)
+    htt = ev()
+    for e in range(4):
+        inc(htt, v.transpose(T.TT[:, :, e:16:4, :], T.SW[:, e:512:4]))
+    ja, jb, jc, jd = [(r // 2) ^ k for k in (3, 2, 1, 0)]
+    parts = [[(ja, ja + 1)], [(a, b) for a, b in ((0, ja), (ja + 1, 4)) if a < b]]
+    steps = [
+        lambda a, b: [v.tensor_tensor(T.P[:, a:b], T.TT[:, a:b, 0:8, 0:4], T.TT[:, a:b, 8:16, 0:4], add)],
+        lambda a, b: [v.tensor_tensor(T.H[0:64, a:b], T.P[0:64, a:b], T.P[64:128, a:b], add)],
+        lambda a, b: [v.tensor_tensor(T.K[0:32, a:b], T.H[0:32, a:b], T.H[32:64, a:b], add)],
+        lambda a, b: [v.transpose(T.ZT[k:k + 32, a:b], T.K[0:32, a:b]) for k in (0, 32)],
+        lambda a, b: [v.tensor_scalar(T.OT[k:k + 64, 32 * a:32 * b], T.ZT[0:64, a:b], 4.0, T.EB[0:64, 0:1], mult, add)
+                      for k in (0, 64)]]
+    hot = [htt, htt]
+    need("v", heb)
+    for step in steps:
+        for i in range(2):
+            need("v", hot[i])
+            hot[i] = ev()
+            for a, b in parts[i]:
+                for ins in step(a, b):
+                    inc(hot[i], ins)
 
-    hpl = [None] * 4
-
-    def plane(q, e):
-        need(q, *hx)
-        out, inp = T.PL[:, 512 * e:512 * e + 512], T.XB[:, e:2048:4]
-        hpl[e] = one(v.tensor_copy(out, inp) if q == "v" else s.activation(out, inp, Copy))
-
-    plane("s", 3); plane("s", 2)
-    plane("v", 0); plane("v", 1)
-    need("v", hw)
-    hwq = one(v.quantize_mx(T.WQ[:], T.WS[:], T.WB[:]))
-    need("v", hr)
-    htt = one(v.transpose(T.TT[:], T.R[:]))
-    hsn, hot = {}, {}
-
-    def sums(j):
-        need("v", htt, hm8)
-        hsn[j] = one(v.tensor_tensor_scan(T.SN[:, 64 * j:64 * j + 64], T.M8[:], T.TT[:, j:256:4], 0.0, mult, add))
-
-    def listed(j):
-        need("v", hsn[j])
-        hot[j] = one(v.tensor_scalar(T.OT[:, 8 * j:8 * j + 8], T.SN[:, 64 * j + 7:64 * j + 64:8], 256.0, None, add))
-
-    def gather(q, h, run, n, slot, es):
-        for e in es:
-            need(q, hot[run // 2], hpl[e])
-            out = T.G[:, 256 * slot + e:256 * (slot + n):4]
-            win = T.PL[:, 512 * e:512 * e + 512].indirect(T.OT[:, 4 * run:4 * (run + n)])
-            inc(h, v.tensor_copy(out, win) if q == "v" else s.activation(out, win, Copy))
-        return h
+    def gather(q, run, slot, k0, k1):
+        need(q, hot[run // 2 != ja], *hx)
+        out = T.G[:, 256 * slot + 16 * k0:256 * slot + 16 * k1]
+        win = T.XB[:, 0:2048].indirect(T.OT[:, 16 * run + k0:16 * run + k1])
+        return one(v.tensor_copy(out, win) if q == "v" else s.activation(out, win, Copy))
 
     def stage(run, n, slot, nv):
-        return gather("v", ev(), run, n, slot, range(nv)), gather("s", ev(), run, n, slot, range(nv, 4))
+        return gather("v", run, slot, 0, nv), gather("s", run, slot, nv, 16 * n)
 
     def quant(slot, c, hs):
         need("v", *hs)
         return one(v.quantize_mx(T.GQ[:, c:c + 128], T.GS[:, c:c + 128], T.G[:, 256 * slot:256 * slot + 512]))
 
-    ja, jb, jc, jd = [(r // 2) ^ k for k in (3, 2, 1, 0)]
     partner = r ^ 1
-    sums(ja); sums(jb); listed(ja); listed(jb)
-    hA = stage(2 * ja, 2, 0, 2)
-    sums(jc)
+    hA = stage(2 * ja, 2, 0, 16)
+    hB = stage(2 * jb, 2, 2, 14)
     hq1 = quant(0, 0, hA)
-    listed(jc)
-    hB = stage(2 * jb, 2, 2, 1)
-    hC = gather("v", ev(), 2 * jc, 2, 4, (0,)), gather("s", ev(), 2 * jc, 2, 4, (2, 3))
-    sums(jd)
+    hC = stage(2 * jc, 2, 4, 14)
     hq2 = quant(2, 128, hB)
-    listed(jd)
-    gather("v", hC[0], 2 * jc, 2, 4, (1,))
-    hD = gather("v", ev(), partner, 1, 6, (0,)), gather("s", ev(), partner, 1, 6, (2, 3))
+    hD = stage(partner, 1, 6, 8)
     hq3 = quant(4, 256, hC)
-    gather("v", hD[0], partner, 1, 6, (1,))
+    need("v", hw)
+    hwq = one(v.quantize_mx(T.WQ[:], T.WS[:], T.WB[:]))
     hq4 = quant(5, 384, hD)
-    hq5 = quant(6, 512, stage(r, 1, 7, 1))
-    h = one(v.tensor_copy(T.HB[:], T.SN[:, 7:256:8]))
-    need("v", h)
-    h = one(v.transpose(T.IV[:], T.HB[:]))
-    need("v", h)
-    hif = one(v.tensor_scalar(T.IF[:], T.IV[:, 0:16], 256.0, None, add))
+    hif = one(v.tensor_scalar(T.IF[0:32], T.K[0:32, jd, 0:16:4], 256.0, None, add))
+    hq5 = quant(6, 512, [gather("s", r, 7, 0, 16)])
 
     nsent = [0]
 
@@ -294,8 +265,7 @@ def rank_program(g, core, T, topo):
         for i, (d, srcs, dst) in enumerate(parts):
             rid, pid, _se = topo.addr(T.cores[d])
             e = topo.engines(core, T.cores[d])
-            w = len(e) // len(parts)
-            e = e[w * i:w * i + w] if i + 1 < len(parts) else e[w * i:]
+            e = e[i::2] if len(parts) == 2 else e[i:i + 1] if i + 1 < len(parts) else e[i:]
             ts.append(RemoteDMATransfer(dst_ids=[DstId(rid=rid, pnc=pid)], dma_engine_mask=sum(1 << k for k in e),
                                         remote_sem=sem, srcs=srcs, dsts=[dst], alu_op=int(len(srcs) > 1)))
             nsent[0] += len(e)
@@ -308,7 +278,7 @@ def rank_program(g, core, T, topo):
 
     dA, dB, dC = [[2 * j, 2 * j + 1] for j in (ja, jb, jc)]
     need("g", hid)
-    fused([(d, [T.IXD[1024 * k + 128 * d:1024 * k + 128 * d + 128, :] for k in range(8)], T.IXL[r])
+    fused([(d, [T.IXD[512 * k + 128 * (d // 2):512 * k + 128 * (d // 2) + 128, :] for k in range(8)], T.IXL[r])
            for d in dA + dB + dC + [partner]], T.sem.arrX)
     send(hq1, dA, 0, T.LAQ, T.LAS, CH * (r % 4), T.sem.arrA)
     send(hq2, dB, 128, T.LAQ, T.LAS, CH * (r % 4), T.sem.arrB)
@@ -327,31 +297,25 @@ def rank_program(g, core, T, topo):
         one(sy.dma_start(T.y[:, 128 * lo:128 * hi], T.Y[:, lo:hi]), 16)
         return hs
 
-    others = [(a, b) for a, b in ((0, r), (r + 1, N)) if a < b]
-    hnb = ev()
-    sy.wait_ge(T.sem.arrX, 8)
-    need("y", hnz)
+    g.wait_ge(T.sem.arrX, 8)
+    need("g", hfill)
     for a, b in others:
-        inc(hnb, sy.dma_start(T.NB[a:b], T.IXL[a:b, :, 0]), 16)
+        one(g.dma_start(T.ix[a:b, :], T.IXL[a:b, CH * (r % 2):CH * (r % 2) + CH, 0], accum_op=add), 16)
     need("y", hif)
-    one(sy.dma_start(T.ix[r:r + 1, :], T.IF[4 * r:4 * r + 4, :]), 16)
+    one(sy.dma_start(T.ix[r:r + 1, :], T.IF[16 * (r % 2):16 * (r % 2) + 16, :]), 16)
 
-    need("t", hwq, hq5)
-    hown = finish(r, r + 1, CH, ((T.VB0, 0), (T.SB0, 0)), T.GQ, T.GS, 512)
+    need("t", hwq)
     te.wait_ge(T.sem.arrA, 16)
-    finish(dA[0], dA[0] + 2, 0, ((T.SC, 0), (T.SC, 512)), T.LAQ, T.LAS, CH * (dA[0] % 4))
-    need("v", hnb)
-    h = one(v.tensor_scalar(T.NF[0:N], T.NB[0:N, :, 0:16], 256.0, None, add))
-    need("y", h)
-    for a, b in others:
-        one(sy.dma_start(T.ix[a:b, :], T.NF[a:b]), 16)
-    need("t", *hown)
+    hfa = finish(dA[0], dA[0] + 2, 0, ((T.SC, 0), (T.SC, 512)), T.LAQ, T.LAS, CH * (dA[0] % 4))
+    need("t", hq5)
+    finish(r, r + 1, CH, ((T.VB1, 0), (T.SB1, 0)), T.GQ, T.GS, 512)
     te.wait_ge(T.sem.arrB, 16)
     finish(dB[0], dB[0] + 2, 0, ((T.VB0, 0), (T.SB0, 0)), T.LAQ, T.LAS, CH * (dB[0] % 4))
     te.wait_ge(T.sem.arrC, 16)
     finish(dC[0], dC[0] + 2, 0, ((T.SC, 1024), (T.SC, 1536)), T.LBQ, T.LBS, 0)
+    need("t", *hfa)
     te.wait_ge(T.sem.arrD, 16)
-    finish(partner, partner + 1, CH, ((T.VB1, 0), (T.SB1, 0)), T.LBQ, T.LBS, 64)
+    finish(partner, partner + 1, CH, ((T.SC, 0), (T.SC, 512)), T.LBQ, T.LBS, 64)
 
     g.wait_ge(T.sem.sent, nsent[0])
     for h in events:

@@ -4,7 +4,8 @@ from concourse.mybir import dt, AluOpType, ActivationFunctionType
 N, TC, O, CH = 8, 512, 2, 64
 MX4 = "float8_e4m3fn_x4"
 SCRATCH = {
-    "UB": ("sbuf", [128, 16], "bfloat16"),
+    "UN": ("sbuf", [128, 512], "bfloat16"),
+    "NQ": ("sbuf", [128, 128], MX4), "NS": ("sbuf", [128, 128], "uint8"),
     "UR": ("sbuf", [128, 512], "bfloat16"),
     "UQ": ("sbuf", [128, 128], MX4), "US": ("sbuf", [128, 128], "uint8"),
     "XB": ("sbuf", [128, 2048], "bfloat16"),
@@ -16,13 +17,13 @@ SCRATCH = {
     "PF": ("sbuf", [128, 4], "float32"), "FB": ("sbuf", [128, 8], "bfloat16"),
     "EB": ("sbuf", [128, 8], "float32"),
     "JF": ("sbuf", [128, 64], "float32"), "J": ("sbuf", [128, 64], "bfloat16"),
-    "MK": ("sbuf", [128, 3, 392], "bfloat16"),
+    "MK": ("sbuf", [128, 520], "bfloat16"),
     "SCS": ("sbuf", [128, 2], "float32"),
     "SG": ("sbuf", [128, 4, 256], "bfloat16"),
     "AB": ("sbuf", [128, 2, 264], "bfloat16"),
     "AC": ("sbuf", [128, 4], "float32"),
-    "C": ("sbuf", [128, 6, 256], "bfloat16"),
-    "QS": ("sbuf", [128, 8, 264], "bfloat16"),
+    "C": ("sbuf", [128, 2, 640], "bfloat16"),
+    "QS": ("sbuf", [128, 6, 264], "bfloat16"),
     "PK": ("sbuf", [128, 2], "bfloat16"),
     "OF": ("sbuf", [128, 8], "uint16"),
     "SW": ("sbuf", [128, 512], "bfloat16"),
@@ -30,8 +31,8 @@ SCRATCH = {
     "P": ("sbuf", [128, 4, 32], "bfloat16"), "H": ("sbuf", [128, 4, 32], "bfloat16"),
     "K": ("sbuf", [128, 4, 32], "bfloat16"), "ZT": ("sbuf", [128, 4, 32], "bfloat16"),
     "OT": ("sbuf", [128, 128], "uint16"),
-    "G": ("sbuf", [128, 2048], "bfloat16"),
-    "GQ": ("sbuf", [128, 640], MX4), "GS": ("sbuf", [128, 640], "uint8"),
+    "G": ("sbuf", [128, 2304], "bfloat16"),
+    "GQ": ("sbuf", [128, 768], MX4), "GS": ("sbuf", [128, 768], "uint8"),
     "LAQ": ("sbuf", [128, 256], MX4), "LAS": ("sbuf", [128, 256], "uint8"),
     "LBQ": ("sbuf", [128, 192], MX4), "LBS": ("sbuf", [128, 192], "uint8"),
     "IF": ("sbuf", [128, 4], "float32"),
@@ -87,9 +88,9 @@ def rank_program(g, core, T, topo):
                 Q[q].wait_ge(T.sem["e%d" % h[0]], h[1])
 
     hx = [None] * 4
-    hu = one(sy.dma_start(T.UB[:], T.u[:, 0:16]), 16)
-    for a in range(4):
-        hx[a] = one((sy if a % 2 else s).dma_start(T.XB[:, 512 * a:512 * a + 512], T.x[:, 512 * a:512 * a + 512]), 16)
+    hu = one(sy.dma_start(T.UN[:, 0:16], T.u[:, 0:16]), 16)
+    for q, a, b in ((s, 0, 1), (sy, 1, 2), (s, 2, 3), (sy, 3, 4)):
+        hx[a:b] = [one(q.dma_start(T.XB[:, 512 * a:512 * b], T.x[:, 512 * a:512 * b]), 16)] * (b - a)
     need("y", *hx)
     hw = one(sy.dma_start(T.WB[:], T.w[:]), 16)
 
@@ -99,13 +100,15 @@ def rank_program(g, core, T, topo):
     hpi = one(g.iota(T.PI[:], [[0, 32]], 0, 1))
     hpf = one(iota(T.PF[:], [[1664 - 2296, 2], [638 - 2296, 2]], 2296, 1))
     hjf = one(iota(T.JF[:], [[128, 4], [1, 16]], -256 - 2304))
+    hone = one(v.memset(T.MK[:], 1.0))
+    hgz = one(v.memset(T.G[:, 0:256], 0.0))
     need("v", hpi)
     hui = one(v.tensor_scalar(T.UI[:], T.PI[:], 3, None, AluOpType.bitwise_and))
-    hone = one(v.memset(T.MK[:], 1.0))
+    hun = one(v.memset(T.UN[:, 16:512], 0.0))
     need("g", hone)
     hm = ev()
-    for k, (c, fill, step, base) in enumerate(((129, -1.0, -1, 0), (0, 0.0, -1, 0), (0, 0.0, 1, -127))):
-        inc(hm, g.affine_select(T.MK[:, k, c:c + 128], T.MK[:, k, c:c + 128], [[1, 128]], ne, fill, base, step))
+    for c, fill, step, base in ((129, -1.0, -1, 0), (385, 0.0, 1, -127)):
+        inc(hm, g.affine_select(T.MK[:, c:c + 128], T.MK[:, c:c + 128], [[1, 128]], ne, fill, base, step))
     hpk = one(iota(T.PK[:], [[-256, 2]], 0, -2))
     hsw = one(iota(T.SW[:], [[0, 512]], 0))
     hnz = one(iota(T.NF[0:N], [[0, 64]], 256))
@@ -121,120 +124,152 @@ def rank_program(g, core, T, topo):
     for a, b in others:
         inc(hfill, sy.dma_start(T.ix[a:b, :], T.NF[a:b]), 16)
     need("s", huo, hu)
-    hur1 = one(s.activation(T.UR[:, 224:512], T.UB[:, 0:16].indirect(T.UO[:, 14:32]), Copy))
-    need("v", huo, hu)
-    hur0 = one(v.tensor_copy(T.UR[:, 0:224], T.UB[:, 0:16].indirect(T.UO[:, 0:14])))
+    hur1 = one(s.activation(T.UR[:, 192:512], T.UN[:, 0:16].indirect(T.UO[:, 12:32]), Copy))
+    need("v", hun, hu)
+    hnq = one(v.quantize_mx(T.NQ[:], T.NS[:], T.UN[:]))
+    need("v", huo)
+    hur0 = one(v.tensor_copy(T.UR[:, 0:192], T.UN[:, 0:16].indirect(T.UO[:, 0:12])))
 
     hq, hsc, hvb, hsb = [None] * 4, [None] * 4, [None] * 2, [None] * 2
     huq = ev()
 
-    def quant_x(a):
-        need("v", hx[a])
-        hq[a] = one(v.quantize_mx(T.XQ[:, 128 * a:128 * a + 128], T.XS[:, 128 * a:128 * a + 128],
-                                  T.XB[:, 512 * a:512 * a + 512]))
+    def quant_x(a, b):
+        need("v", *hx[a:b])
+        hq[a:b] = [one(v.quantize_mx(T.XQ[:, 128 * a:128 * b], T.XS[:, 128 * a:128 * b], T.XB[:, 512 * a:512 * b]))] * (b - a)
 
     def score_col(a):
-        need("t", huq, hq[a])
+        need("t", hnq, hq[a])
         hsc[a] = one(te.matmul_mx(T.SC[:, 512 * a:512 * a + 128], T.XQ[:, 128 * a:128 * a + 128],
-                                  T.XS[:, 128 * a:128 * a + 128], T.UQ[:], T.US[:], True, True))
+                                  T.XS[:, 128 * a:128 * a + 128], T.NQ[:], T.NS[:], True, True))
 
     def score_row(bank, b):
         need("t", huq, hq[2 * b], hq[2 * b + 1])
         return one(te.matmul_mx(T[bank % b][:, 0:256], T.UQ[:], T.US[:], T.XQ[:, 256 * b:256 * b + 256],
                                 T.XS[:, 256 * b:256 * b + 256], True, True))
 
-    quant_x(0)
+    quant_x(0, 1)
+    score_col(0)
+    quant_x(1, 2)
+    score_col(1)
     need("v", hur0, hur1)
     inc(huq, v.quantize_mx(T.UQ[:], T.US[:], T.UR[:]))
-    score_col(0)
-    quant_x(1)
-    score_col(1)
-    hvb[0] = score_row("VB%d", 0)
-    quant_x(2)
-    score_col(2)
     hsb[0] = score_row("SB%d", 0)
-    quant_x(3)
+    hvb[0] = score_row("VB%d", 0)
+    quant_x(2, 3)
+    score_col(2)
+    quant_x(3, 4)
     score_col(3)
     hvb[1] = score_row("VB%d", 1)
     hsb[1] = score_row("SB%d", 1)
 
-    need("s", hsc[0], hsc[1])
-    hcol = one(s.activation(T.SCS[:], T.SC[:, 0:1024:512], Copy))
+    hcol = []
+    for a in range(2):
+        need("s", hsc[a])
+        hcol.append(one(s.activation(T.SCS[:, a:a + 1], T.SC[:, 512 * a:512 * a + 1], Copy)))
     need("s", hjf)
     hj = one(s.activation(T.J[:], T.JF[:], F.Identity, bias=T.FB[:, 0:1]))
 
     def signs(a, b, **kw):
-        need("s", hcol, hsb[b])
+        need("s", hcol[a], hsb[b])
         return one(s.activation(T.SG[:, 2 * b + a, :], T["SB%d" % b][:, 0:256], F.Sign, bias=T.SCS[:, a:a + 1], scale=-1.0, **kw))
 
     hsg = [signs(a, 0, accum_out=T.AC[:, a:a + 1]) for a in range(2)]
-    hab = []
-    for a in range(2):
-        need("s", hsg[a])
-        hab.append(one(s.activation(T.AB[:, a, 1:257], T.SG[:, a, :], F.Abs)))
+    need("s", hsg[0])
+    hab = [one(s.activation(T.AB[:, 0, 1:257], T.SG[:, 0, :], F.Abs))]
+    need("s", hsg[1])
+    hac = one(s.activation(T.AB[:, :, 0], T.AC[:, 0:2], Copy))
     hup = [signs(a, 1) for a in range(2)]
     hct = []
     for a in range(2):
         need("s", hup[a])
         hct.append(one(s.activation(T.SG[:, 2 + a, :], T.SG[:, 2 + a, :], F.Relu, scale=-1.0, accum_out=T.AC[:, 2 + a:3 + a])))
 
-    def flags(k, a, b, view, op):
+    def flags(a, c, b, view, op):
         need("v", hvb[b], hsc[a])
-        return one(v.tensor_scalar(T.C[:, k, 0:view.shape[1]], view, T.SC[:, 512 * a:512 * a + 1], None, op))
+        return one(v.tensor_scalar(T.C[:, a - 2, c:c + view.shape[1]], view, T.SC[:, 512 * a:512 * a + 1], None, op))
 
     def scan(k, n, d0, d1, first, op, *hs):
         need("v", *hs)
         return one(v.tensor_tensor_scan(T.QS[:, k, 264 - n:264], d0, d1, first, add, op))
 
-    hf = [flags(0, 2, 0, T.VB0[:, 0:256], ge), flags(1, 3, 0, T.VB0[:, 0:256], ge),
-          flags(2, 2, 1, T.VB1[:, 0:256], gt), flags(3, 3, 1, T.VB1[:, 255::-1], ge),
-          flags(4, 2, 1, T.VB1[:, 127::-1], ge), flags(5, 3, 1, T.VB1[:, 128:256], gt)]
-    need("v", *hsg)
-    hac = one(v.tensor_copy(T.AB[:, :, 0], T.AC[:, 0:2]))
-    hs = [scan(k, 128, T.C[:, k, 0:128], T.C[:, k, 128:256], 0.0, add, hf[k]) for k in range(2)]
-    hs += [scan(k, n, T.C[:, k, 0:n], T.MK[:, m, 0:n], 0.0, mult, hf[k], hm)
-           for k, n, m in ((2, 256, 1), (3, 256, 2), (4, 128, 2), (5, 128, 1))]
-    hs += [scan(6 + a, 257, T.AB[:, a, 0:257], T.MK[:, 0, 128 - 128 * a:385 - 128 * a], T.PK[:, a:a + 1], mult, hac, hab[a], hpk)
-           for a in range(2)]
+    eq = AluOpType.is_equal
+    f20, f30 = flags(2, 0, 0, T.VB0[:, 0:256], ge), flags(3, 0, 0, T.VB0[:, 0:256], ge)
+    e3, e2 = flags(3, 512, 1, T.VB1[:, 255:127:-1], eq), flags(2, 512, 1, T.VB1[:, 127::-1], eq)
+    f31 = flags(3, 256, 1, T.VB1[:, 0:128], ge)
+    f21 = flags(2, 256, 1, T.VB1[:, 0:256], gt)
+    f32 = flags(3, 384, 1, T.VB1[:, 128:256], gt)
+    need("v", hsg[1])
+    hab.append(one(v.tensor_scalar(T.AB[:, 1, 1:257], T.SG[:, 1, :], 0.0, None, ne)))
+
+    def late(a):
+        return scan(a, 257, T.AB[:, a, 0:257], T.MK[:, 128 - 128 * a:385 - 128 * a], T.PK[:, a:a + 1], mult, hac, hab[a], hpk)
+
+    e2 = scan(4, 128, T.C[:, 0, 512:640], T.MK[:, 385:513], 0.0, mult, e2, hm)
+    t2 = scan(2, 256, T.C[:, 0, 0:256], T.C[:, 0, 256:512], -256.0, add, f20, f21)
+    l0 = late(0)
+    t3 = scan(3, 256, T.C[:, 1, 0:256], T.C[:, 1, 256:512], -256.0, add, f30, f31, f32)
+    e3 = scan(5, 128, T.C[:, 1, 512:640], T.MK[:, 385:513], 0.0, mult, e3)
+    l1 = late(1)
     hof = ev()
-    for a in range(2):
-        need("v", hs[a], hs[2 + a], hs[4 + a])
-        inc(hof, v.tensor_scalar(T.OF[:, 2 + a:3 + a], T.QS[:, a, 263:264], T.QS[:, 2 + a, 263:264], T.QS[:, 4 + a, 263:264], add, add))
-    for a in range(2):
-        need("v", hs[6 + a], hct[a])
-        inc(hof, v.tensor_scalar(T.OF[:, a:a + 1], T.QS[:, 6 + a, 263:264], 0.5, T.AC[:, 2 + a:3 + a], mult, add))
+    for a, hh in ((0, (l0, hct[0])), (2, (t2, e2)), (3, (t3, e3)), (1, (l1, hct[1]))):
+        need("v", *hh)
+        if a < 2:
+            inc(hof, v.tensor_scalar(T.OF[:, a:a + 1], T.QS[:, a, 263:264], 0.5, T.AC[:, 2 + a:3 + a], mult, add))
+        else:
+            inc(hof, v.tensor_scalar(T.OF[:, a:a + 1], T.QS[:, a, 263:264], T.QS[:, 2 + a, 263:264], 256.0, add, add))
+    hwq = ev()
+
+    def quant_w(o):
+        need("v", hw)
+        inc(hwq, v.quantize_mx(T.WQ[:, 128 * o:128 * o + 128], T.WS[:, 128 * o:128 * o + 128], T.WB[:, 512 * o:512 * o + 512]))
+
+    quant_w(0)
     need("v", hof, hsw, hj)
     hwin = one(v.tensor_copy(T.SW[:, 0:512].indirect(T.OF[:, 0:4]), T.J[:]))
+    quant_w(1)
 
+    ja, jb, jc, jd = [(r // 2) ^ k for k in (3, 2, 1, 0)]
     need("y", hwin)
     hid = one(sy.dma_start(T.IXD[:, 0], T.SW[0:128:16, :]), 16)
     need("v", hwin)
     htt = ev()
     for e in range(4):
         inc(htt, v.transpose(T.TT[:, :, e:16:4, :], T.SW[:, e:512:4]))
-    ja, jb, jc, jd = [(r // 2) ^ k for k in (3, 2, 1, 0)]
-    parts = [[(ja, ja + 1)], [(a, b) for a, b in ((0, ja), (ja + 1, 4)) if a < b]]
+    parts = [[(0, 1)], [(1, 4)]]
+
+    def halves(a, b):
+        lo, hi = a ^ ja, (b - 1) ^ ja
+        q = slice(lo, hi + 1) if lo <= hi else slice(lo, hi - 1 if hi else None, -1)
+        w = 16 if a else 32
+        return v.tensor_tensor(T.P[:, a:b, 0:w], T.TT[:, q, 0:w // 4, 0:4], T.TT[:, q, 8:8 + w // 4, 0:4], add)
+
     steps = [
-        lambda a, b: [v.tensor_tensor(T.P[:, a:b], T.TT[:, a:b, 0:8, 0:4], T.TT[:, a:b, 8:16, 0:4], add)],
-        lambda a, b: [v.tensor_tensor(T.H[0:64, a:b], T.P[0:64, a:b], T.P[64:128, a:b], add)],
-        lambda a, b: [v.tensor_tensor(T.K[0:32, a:b], T.H[0:32, a:b], T.H[32:64, a:b], add)],
+        lambda a, b: [halves(a, b)] if a == 0 else [halves(1, 2), halves(2, 4)],
+        lambda a, b: [v.tensor_tensor(T.H[0:64, a:b, 0:w], T.P[0:64, a:b, 0:w], T.P[64:128, a:b, 0:w], add)
+                      for w in (16 if a else 32,)],
+        lambda a, b: [v.tensor_tensor(T.K[0:32, a:b, c:c + w], T.H[0:32, a:b, 0:w], T.H[32:64, a:b, 0:w], add)
+                      for c, w in (((0, 16), (16, 16)) if a else ((0, 32),))],
         lambda a, b: [v.transpose(T.ZT[k:k + 32, a:b], T.K[0:32, a:b]) for k in (0, 32)],
         lambda a, b: [v.tensor_scalar(T.OT[k:k + 64, 32 * a:32 * b], T.ZT[0:64, a:b], 4.0, T.EB[0:64, 0:1], mult, add)
                       for k in (0, 64)]]
     hot = [htt, htt]
     need("v", heb)
-    for step in steps:
-        for i in range(2):
-            need("v", hot[i])
-            hot[i] = ev()
-            for a, b in parts[i]:
-                for ins in step(a, b):
-                    inc(hot[i], ins)
+
+    def step(i, k):
+        need("v", hot[i])
+        hot[i] = ev()
+        for a, b in parts[i]:
+            for ins in steps[k](a, b):
+                inc(hot[i], ins)
+
+    for k in range(5):
+        step(0, k)
+        step(1, k)
 
     def gather(q, run, slot, k0, k1):
         need(q, hot[run // 2 != ja], *hx)
         out = T.G[:, 256 * slot + 16 * k0:256 * slot + 16 * k1]
-        win = T.XB[:, 0:2048].indirect(T.OT[:, 16 * run + k0:16 * run + k1])
+        win = T.XB[:, 0:2048].indirect(T.OT[:, 16 * (run ^ 2 * ja) + k0:16 * (run ^ 2 * ja) + k1])
         return one(v.tensor_copy(out, win) if q == "v" else s.activation(out, win, Copy))
 
     def stage(run, n, slot, nv):
@@ -245,18 +280,19 @@ def rank_program(g, core, T, topo):
         return one(v.quantize_mx(T.GQ[:, c:c + 128], T.GS[:, c:c + 128], T.G[:, 256 * slot:256 * slot + 512]))
 
     partner = r ^ 1
-    hA = stage(2 * ja, 2, 0, 16)
-    hB = stage(2 * jb, 2, 2, 14)
-    hq1 = quant(0, 0, hA)
-    hC = stage(2 * jc, 2, 4, 14)
-    hq2 = quant(2, 128, hB)
-    hD = stage(partner, 1, 6, 8)
-    hq3 = quant(4, 256, hC)
-    need("v", hw)
-    hwq = one(v.quantize_mx(T.WQ[:], T.WS[:], T.WB[:]))
-    hq4 = quant(5, 384, hD)
-    hif = one(v.tensor_scalar(T.IF[0:32], T.K[0:32, jd, 0:16:4], 256.0, None, add))
-    hq5 = quant(6, 512, [gather("s", r, 7, 0, 16)])
+    h0 = stage(r ^ 6, 1, 1, 8)
+    h1 = stage(r ^ 7, 1, 2, 12)
+    hq0 = quant(0, 0, h0 + (hgz,))
+    hB = stage(2 * jb, 2, 3, 8)
+    hq1 = quant(1, 128, h1)
+    hC = stage(2 * jc, 2, 5, 10)
+    hq2 = quant(3, 256, hB)
+    hD = stage(partner, 1, 7, 10)
+    hq3 = quant(5, 384, hC)
+    hq4 = quant(6, 512, hD)
+    hown = gather("s", r, 8, 0, 16)
+    hif = one(v.tensor_scalar(T.IF[0:32], T.K[0:32, jd ^ ja, 0:16:4], 256.0, None, add))
+    hq5 = quant(7, 640, [hown])
 
     nsent = [0]
 
@@ -280,19 +316,20 @@ def rank_program(g, core, T, topo):
     need("g", hid)
     fused([(d, [T.IXD[512 * k + 128 * (d // 2):512 * k + 128 * (d // 2) + 128, :] for k in range(8)], T.IXL[r])
            for d in dA + dB + dC + [partner]], T.sem.arrX)
-    send(hq1, dA, 0, T.LAQ, T.LAS, CH * (r % 4), T.sem.arrA)
-    send(hq2, dB, 128, T.LAQ, T.LAS, CH * (r % 4), T.sem.arrB)
-    send(hq3, dC, 256, T.LBQ, T.LBS, CH * (r % 2), T.sem.arrC)
-    send(hq4, [partner], 448, T.LBQ, T.LBS, 128, T.sem.arrD)
+    send(hq0, [r ^ 6], 64, T.LAQ, T.LAS, CH * (r % 4), T.sem.arrA)
+    send(hq1, [r ^ 7], 192, T.LAQ, T.LAS, CH * (r % 4), T.sem.arrA)
+    send(hq2, dB, 256, T.LAQ, T.LAS, CH * (r % 4), T.sem.arrB)
+    send(hq3, dC, 384, T.LBQ, T.LBS, CH * (r % 2), T.sem.arrC)
+    send(hq4, [partner], 576, T.LBQ, T.LBS, 128, T.sem.arrD)
 
     def finish(lo, hi, c0, banks, bufq, bufs, c):
         hp = [one(te.matmul_mx(buf[:, at:at + 128], T.WQ[:, 128 * o:128 * o + 128], T.WS[:, 128 * o:128 * o + 128],
                                bufq[:, c:c + 128], bufs[:, c:c + 128], True, True)) for o, (buf, at) in enumerate(banks)]
         hs = []
         for o, (buf, at) in enumerate(banks):
-            need("vs"[o], hp[o])
+            need("sv"[o], hp[o])
             dst, inp = T.Y[:, lo:hi, o, :], buf[:, at + c0:at + c0 + CH * (hi - lo)]
-            hs.append(one(v.tensor_copy(dst, inp) if o == 0 else s.activation(dst, inp, Copy)))
+            hs.append(one(v.tensor_copy(dst, inp) if o else s.activation(dst, inp, Copy)))
         need("y", *hs)
         one(sy.dma_start(T.y[:, 128 * lo:128 * hi], T.Y[:, lo:hi]), 16)
         return hs
@@ -304,13 +341,13 @@ def rank_program(g, core, T, topo):
     need("y", hif)
     one(sy.dma_start(T.ix[r:r + 1, :], T.IF[16 * (r % 2):16 * (r % 2) + 16, :]), 16)
 
-    need("t", hwq)
-    te.wait_ge(T.sem.arrA, 16)
+    need("t", hwq, hwin)
+    te.wait_ge(T.sem.arrA, 32)
     hfa = finish(dA[0], dA[0] + 2, 0, ((T.SC, 0), (T.SC, 512)), T.LAQ, T.LAS, CH * (dA[0] % 4))
-    need("t", hq5)
-    finish(r, r + 1, CH, ((T.VB1, 0), (T.SB1, 0)), T.GQ, T.GS, 512)
     te.wait_ge(T.sem.arrB, 16)
     finish(dB[0], dB[0] + 2, 0, ((T.VB0, 0), (T.SB0, 0)), T.LAQ, T.LAS, CH * (dB[0] % 4))
+    need("t", hq5)
+    finish(r, r + 1, CH, ((T.VB1, 0), (T.SB1, 0)), T.GQ, T.GS, 640)
     te.wait_ge(T.sem.arrC, 16)
     finish(dC[0], dC[0] + 2, 0, ((T.SC, 1024), (T.SC, 1536)), T.LBQ, T.LBS, 0)
     need("t", *hfa)

from concourse.bass import DstId, RemoteDMATransfer
from concourse.mybir import dt, AluOpType, ActivationFunctionType

N, TC, O, CH = 8, 512, 2, 64
MX4 = "float8_e4m3fn_x4"
SCRATCH = {
    "UN": ("sbuf", [128, 512], "bfloat16"),
    "NQ": ("sbuf", [128, 128], MX4), "NS": ("sbuf", [128, 128], "uint8"),
    "UR": ("sbuf", [128, 512], "bfloat16"),
    "UQ": ("sbuf", [128, 128], MX4), "US": ("sbuf", [128, 128], "uint8"),
    "XB": ("sbuf", [128, 2048], "bfloat16"),
    "XQ": ("sbuf", [128, 512], MX4), "XS": ("sbuf", [128, 512], "uint8"),
    "WB": ("sbuf", [128, 1024], "bfloat16"),
    "WQ": ("sbuf", [128, 256], MX4), "WS": ("sbuf", [128, 256], "uint8"),
    "PI": ("sbuf", [128, 32], "int32"),
    "UI": ("sbuf", [128, 32], "int32"), "UO": ("sbuf", [128, 32], "uint16"),
    "PF": ("sbuf", [128, 4], "float32"), "FB": ("sbuf", [128, 8], "bfloat16"),
    "EB": ("sbuf", [128, 8], "float32"),
    "JF": ("sbuf", [128, 64], "float32"), "J": ("sbuf", [128, 64], "bfloat16"),
    "MK": ("sbuf", [128, 520], "bfloat16"),
    "SCS": ("sbuf", [128, 2], "float32"),
    "SG": ("sbuf", [128, 4, 256], "bfloat16"),
    "AB": ("sbuf", [128, 2, 264], "bfloat16"),
    "AC": ("sbuf", [128, 4], "float32"),
    "C": ("sbuf", [128, 2, 640], "bfloat16"),
    "QS": ("sbuf", [128, 6, 264], "bfloat16"),
    "PK": ("sbuf", [128, 2], "bfloat16"),
    "OF": ("sbuf", [128, 8], "uint16"),
    "SW": ("sbuf", [128, 512], "bfloat16"),
    "TT": ("sbuf", [128, 4, 16, 8], "bfloat16"),
    "P": ("sbuf", [128, 4, 32], "bfloat16"), "H": ("sbuf", [128, 4, 32], "bfloat16"),
    "K": ("sbuf", [128, 4, 32], "bfloat16"), "ZT": ("sbuf", [128, 4, 32], "bfloat16"),
    "OT": ("sbuf", [128, 128], "uint16"),
    "G": ("sbuf", [128, 2304], "bfloat16"),
    "GQ": ("sbuf", [128, 768], MX4), "GS": ("sbuf", [128, 768], "uint8"),
    "LAQ": ("sbuf", [128, 256], MX4), "LAS": ("sbuf", [128, 256], "uint8"),
    "LBQ": ("sbuf", [128, 192], MX4), "LBS": ("sbuf", [128, 192], "uint8"),
    "IF": ("sbuf", [128, 4], "float32"),
    "NF": ("sbuf", [128, 64], "float32"),
    "IXD": ("dram", [4096, 1], "bfloat16"), "IXL": ("dram", [8, 128, 1], "bfloat16"),
    "Y": ("sbuf", [128, N, O, CH], "float32"),
    "VB0": ("psum", [128, 512], "float32"), "VB1": ("psum", [128, 512], "float32"),
    "SB0": ("psum", [128, 512], "float32"), "SB1": ("psum", [128, 512], "float32"),
    "SC": ("psum", [128, 2048], "float32"),
}
NEV = 140
SEMAPHORES = ["arrA", "arrB", "arrC", "arrD", "arrX", "sent"] + ["e%d" % i for i in range(NEV)]


def codes(buf, c):
    return buf[:, c:c + CH].bitcast(dt.uint8)


def scales(buf, c):
    return buf[:, c:c + CH]


def rank_program(g, core, T, topo):
    r = T.rank_of(core)
    if r is None:
        return
    add, mult = AluOpType.add, AluOpType.mult
    ge, gt, ne = AluOpType.is_ge, AluOpType.is_gt, AluOpType.not_equal
    F = ActivationFunctionType
    Copy = F.Copy
    v, s, te, sy = g.vector, g.scalar, g.tensor, g.sync
    Q = {"g": g, "v": v, "s": s, "t": te, "y": sy}
    events, seen, done = [], set(), set()

    def ev():
        h = [len(events), 0]
        events.append(h)
        return h

    def inc(h, ins, n=1):
        ins.then_inc(T.sem["e%d" % h[0]], n)
        h[1] += n
        return h

    def one(ins, n=1):
        return inc(ev(), ins, n)

    def need(q, *hs):
        for h in hs:
            if (q, h[0]) not in seen:
                seen.add((q, h[0]))
                done.add(h[0])
                Q[q].wait_ge(T.sem["e%d" % h[0]], h[1])

    hx = [None] * 4
    hu = one(sy.dma_start(T.UN[:, 0:16], T.u[:, 0:16]), 16)
    for q, a, b in ((s, 0, 1), (sy, 1, 2), (s, 2, 3), (sy, 3, 4)):
        hx[a:b] = [one(q.dma_start(T.XB[:, 512 * a:512 * b], T.x[:, 512 * a:512 * b]), 16)] * (b - a)
    need("y", *hx)
    hw = one(sy.dma_start(T.WB[:], T.w[:]), 16)

    def iota(out, pattern, base, step=0):
        return g.iota(out, pattern, base, step, allow_small_or_imprecise_dtypes=True)

    hpi = one(g.iota(T.PI[:], [[0, 32]], 0, 1))
    hpf = one(iota(T.PF[:], [[1664 - 2296, 2], [638 - 2296, 2]], 2296, 1))
    hjf = one(iota(T.JF[:], [[128, 4], [1, 16]], -256 - 2304))
    hone = one(v.memset(T.MK[:], 1.0))
    hgz = one(v.memset(T.G[:, 0:256], 0.0))
    need("v", hpi)
    hui = one(v.tensor_scalar(T.UI[:], T.PI[:], 3, None, AluOpType.bitwise_and))
    hun = one(v.memset(T.UN[:, 16:512], 0.0))
    need("g", hone)
    hm = ev()
    for c, fill, step, base in ((129, -1.0, -1, 0), (385, 0.0, 1, -127)):
        inc(hm, g.affine_select(T.MK[:, c:c + 128], T.MK[:, c:c + 128], [[1, 128]], ne, fill, base, step))
    hpk = one(iota(T.PK[:], [[-256, 2]], 0, -2))
    hsw = one(iota(T.SW[:], [[0, 512]], 0))
    hnz = one(iota(T.NF[0:N], [[0, 64]], 256))
    need("v", hui)
    huo = one(v.tensor_copy(T.UO[:], T.UI[:]))
    need("s", hpf)
    hfb = one(s.activation(T.FB[:, 0:2], T.PF[:, 0:2], F.Identity, bias=0.5))
    need("s", hfb)
    heb = one(s.activation(T.EB[:, 0:1], T.FB[:, 1:2], F.Identity, bias=T.PF[:, 2:3], scale=-1.0))
    need("y", hnz)
    others = [(a, b) for a, b in ((0, r), (r + 1, N)) if a < b]
    hfill = ev()
    for a, b in others:
        inc(hfill, sy.dma_start(T.ix[a:b, :], T.NF[a:b]), 16)
    need("s", huo, hu)
    hur1 = one(s.activation(T.UR[:, 192:512], T.UN[:, 0:16].indirect(T.UO[:, 12:32]), Copy))
    need("v", hun, hu)
    hnq = one(v.quantize_mx(T.NQ[:], T.NS[:], T.UN[:]))
    need("v", huo)
    hur0 = one(v.tensor_copy(T.UR[:, 0:192], T.UN[:, 0:16].indirect(T.UO[:, 0:12])))

    hq, hsc, hvb, hsb = [None] * 4, [None] * 4, [None] * 2, [None] * 2
    huq = ev()

    def quant_x(a, b):
        need("v", *hx[a:b])
        hq[a:b] = [one(v.quantize_mx(T.XQ[:, 128 * a:128 * b], T.XS[:, 128 * a:128 * b], T.XB[:, 512 * a:512 * b]))] * (b - a)

    def score_col(a):
        need("t", hnq, hq[a])
        hsc[a] = one(te.matmul_mx(T.SC[:, 512 * a:512 * a + 128], T.XQ[:, 128 * a:128 * a + 128],
                                  T.XS[:, 128 * a:128 * a + 128], T.NQ[:], T.NS[:], True, True))

    def score_row(bank, b):
        need("t", huq, hq[2 * b], hq[2 * b + 1])
        return one(te.matmul_mx(T[bank % b][:, 0:256], T.UQ[:], T.US[:], T.XQ[:, 256 * b:256 * b + 256],
                                T.XS[:, 256 * b:256 * b + 256], True, True))

    quant_x(0, 1)
    score_col(0)
    quant_x(1, 2)
    score_col(1)
    need("v", hur0, hur1)
    inc(huq, v.quantize_mx(T.UQ[:], T.US[:], T.UR[:]))
    hsb[0] = score_row("SB%d", 0)
    hvb[0] = score_row("VB%d", 0)
    quant_x(2, 3)
    score_col(2)
    quant_x(3, 4)
    score_col(3)
    hvb[1] = score_row("VB%d", 1)
    hsb[1] = score_row("SB%d", 1)

    hcol = []
    for a in range(2):
        need("s", hsc[a])
        hcol.append(one(s.activation(T.SCS[:, a:a + 1], T.SC[:, 512 * a:512 * a + 1], Copy)))
    need("s", hjf)
    hj = one(s.activation(T.J[:], T.JF[:], F.Identity, bias=T.FB[:, 0:1]))

    def signs(a, b, **kw):
        need("s", hcol[a], hsb[b])
        return one(s.activation(T.SG[:, 2 * b + a, :], T["SB%d" % b][:, 0:256], F.Sign, bias=T.SCS[:, a:a + 1], scale=-1.0, **kw))

    hsg = [signs(a, 0, accum_out=T.AC[:, a:a + 1]) for a in range(2)]
    need("s", hsg[0])
    hab = [one(s.activation(T.AB[:, 0, 1:257], T.SG[:, 0, :], F.Abs))]
    need("s", hsg[1])
    hac = one(s.activation(T.AB[:, :, 0], T.AC[:, 0:2], Copy))
    hup = [signs(a, 1) for a in range(2)]
    hct = []
    for a in range(2):
        need("s", hup[a])
        hct.append(one(s.activation(T.SG[:, 2 + a, :], T.SG[:, 2 + a, :], F.Relu, scale=-1.0, accum_out=T.AC[:, 2 + a:3 + a])))

    def flags(a, c, b, view, op):
        need("v", hvb[b], hsc[a])
        return one(v.tensor_scalar(T.C[:, a - 2, c:c + view.shape[1]], view, T.SC[:, 512 * a:512 * a + 1], None, op))

    def scan(k, n, d0, d1, first, op, *hs):
        need("v", *hs)
        return one(v.tensor_tensor_scan(T.QS[:, k, 264 - n:264], d0, d1, first, add, op))

    eq = AluOpType.is_equal
    f20, f30 = flags(2, 0, 0, T.VB0[:, 0:256], ge), flags(3, 0, 0, T.VB0[:, 0:256], ge)
    e3, e2 = flags(3, 512, 1, T.VB1[:, 255:127:-1], eq), flags(2, 512, 1, T.VB1[:, 127::-1], eq)
    f31 = flags(3, 256, 1, T.VB1[:, 0:128], ge)
    f21 = flags(2, 256, 1, T.VB1[:, 0:256], gt)
    f32 = flags(3, 384, 1, T.VB1[:, 128:256], gt)
    need("v", hsg[1])
    hab.append(one(v.tensor_scalar(T.AB[:, 1, 1:257], T.SG[:, 1, :], 0.0, None, ne)))

    def late(a):
        return scan(a, 257, T.AB[:, a, 0:257], T.MK[:, 128 - 128 * a:385 - 128 * a], T.PK[:, a:a + 1], mult, hac, hab[a], hpk)

    e2 = scan(4, 128, T.C[:, 0, 512:640], T.MK[:, 385:513], 0.0, mult, e2, hm)
    t2 = scan(2, 256, T.C[:, 0, 0:256], T.C[:, 0, 256:512], -256.0, add, f20, f21)
    l0 = late(0)
    t3 = scan(3, 256, T.C[:, 1, 0:256], T.C[:, 1, 256:512], -256.0, add, f30, f31, f32)
    e3 = scan(5, 128, T.C[:, 1, 512:640], T.MK[:, 385:513], 0.0, mult, e3)
    l1 = late(1)
    hof = ev()
    for a, hh in ((0, (l0, hct[0])), (2, (t2, e2)), (3, (t3, e3)), (1, (l1, hct[1]))):
        need("v", *hh)
        if a < 2:
            inc(hof, v.tensor_scalar(T.OF[:, a:a + 1], T.QS[:, a, 263:264], 0.5, T.AC[:, 2 + a:3 + a], mult, add))
        else:
            inc(hof, v.tensor_scalar(T.OF[:, a:a + 1], T.QS[:, a, 263:264], T.QS[:, 2 + a, 263:264], 256.0, add, add))
    hwq = ev()

    def quant_w(o):
        need("v", hw)
        inc(hwq, v.quantize_mx(T.WQ[:, 128 * o:128 * o + 128], T.WS[:, 128 * o:128 * o + 128], T.WB[:, 512 * o:512 * o + 512]))

    quant_w(0)
    need("v", hof, hsw, hj)
    hwin = one(v.tensor_copy(T.SW[:, 0:512].indirect(T.OF[:, 0:4]), T.J[:]))
    quant_w(1)

    ja, jb, jc, jd = [(r // 2) ^ k for k in (3, 2, 1, 0)]
    need("y", hwin)
    hid = one(sy.dma_start(T.IXD[:, 0], T.SW[0:128:16, :]), 16)
    need("v", hwin)
    htt = ev()
    for e in range(4):
        inc(htt, v.transpose(T.TT[:, :, e:16:4, :], T.SW[:, e:512:4]))
    parts = [[(0, 1)], [(1, 4)]]

    def halves(a, b):
        lo, hi = a ^ ja, (b - 1) ^ ja
        q = slice(lo, hi + 1) if lo <= hi else slice(lo, hi - 1 if hi else None, -1)
        w = 16 if a else 32
        return v.tensor_tensor(T.P[:, a:b, 0:w], T.TT[:, q, 0:w // 4, 0:4], T.TT[:, q, 8:8 + w // 4, 0:4], add)

    steps = [
        lambda a, b: [halves(a, b)] if a == 0 else [halves(1, 2), halves(2, 4)],
        lambda a, b: [v.tensor_tensor(T.H[0:64, a:b, 0:w], T.P[0:64, a:b, 0:w], T.P[64:128, a:b, 0:w], add)
                      for w in (16 if a else 32,)],
        lambda a, b: [v.tensor_tensor(T.K[0:32, a:b, c:c + w], T.H[0:32, a:b, 0:w], T.H[32:64, a:b, 0:w], add)
                      for c, w in (((0, 16), (16, 16)) if a else ((0, 32),))],
        lambda a, b: [v.transpose(T.ZT[k:k + 32, a:b], T.K[0:32, a:b]) for k in (0, 32)],
        lambda a, b: [v.tensor_scalar(T.OT[k:k + 64, 32 * a:32 * b], T.ZT[0:64, a:b], 4.0, T.EB[0:64, 0:1], mult, add)
                      for k in (0, 64)]]
    hot = [htt, htt]
    need("v", heb)

    def step(i, k):
        need("v", hot[i])
        hot[i] = ev()
        for a, b in parts[i]:
            for ins in steps[k](a, b):
                inc(hot[i], ins)

    for k in range(5):
        step(0, k)
        step(1, k)

    def gather(q, run, slot, k0, k1):
        need(q, hot[run // 2 != ja], *hx)
        out = T.G[:, 256 * slot + 16 * k0:256 * slot + 16 * k1]
        win = T.XB[:, 0:2048].indirect(T.OT[:, 16 * (run ^ 2 * ja) + k0:16 * (run ^ 2 * ja) + k1])
        return one(v.tensor_copy(out, win) if q == "v" else s.activation(out, win, Copy))

    def stage(run, n, slot, nv):
        return gather("v", run, slot, 0, nv), gather("s", run, slot, nv, 16 * n)

    def quant(slot, c, hs):
        need("v", *hs)
        return one(v.quantize_mx(T.GQ[:, c:c + 128], T.GS[:, c:c + 128], T.G[:, 256 * slot:256 * slot + 512]))

    partner = r ^ 1
    h0 = stage(r ^ 6, 1, 1, 8)
    h1 = stage(r ^ 7, 1, 2, 12)
    hq0 = quant(0, 0, h0 + (hgz,))
    hB = stage(2 * jb, 2, 3, 8)
    hq1 = quant(1, 128, h1)
    hC = stage(2 * jc, 2, 5, 10)
    hq2 = quant(3, 256, hB)
    hD = stage(partner, 1, 7, 10)
    hq3 = quant(5, 384, hC)
    hq4 = quant(6, 512, hD)
    hown = gather("s", r, 8, 0, 16)
    hif = one(v.tensor_scalar(T.IF[0:32], T.K[0:32, jd ^ ja, 0:16:4], 256.0, None, add))
    hq5 = quant(7, 640, [hown])

    nsent = [0]

    def fused(parts, sem):
        ts = []
        for i, (d, srcs, dst) in enumerate(parts):
            rid, pid, _se = topo.addr(T.cores[d])
            e = topo.engines(core, T.cores[d])
            e = e[i::2] if len(parts) == 2 else e[i:i + 1] if i + 1 < len(parts) else e[i:]
            ts.append(RemoteDMATransfer(dst_ids=[DstId(rid=rid, pnc=pid)], dma_engine_mask=sum(1 << k for k in e),
                                        remote_sem=sem, srcs=srcs, dsts=[dst], alu_op=int(len(srcs) > 1)))
            nsent[0] += len(e)
        g.remote_dma_fused(ts, local_sem=T.sem.sent)

    def send(h, ds, c, bufq, bufs, at, sem):
        need("g", h)
        fused([(d, [codes(T.GQ, c + CH * i)], codes(bufq, at)) for i, d in enumerate(ds)], sem)
        fused([(d, [scales(T.GS, c + CH * i)], scales(bufs, at)) for i, d in enumerate(ds)], sem)

    dA, dB, dC = [[2 * j, 2 * j + 1] for j in (ja, jb, jc)]
    need("g", hid)
    fused([(d, [T.IXD[512 * k + 128 * (d // 2):512 * k + 128 * (d // 2) + 128, :] for k in range(8)], T.IXL[r])
           for d in dA + dB + dC + [partner]], T.sem.arrX)
    send(hq0, [r ^ 6], 64, T.LAQ, T.LAS, CH * (r % 4), T.sem.arrA)
    send(hq1, [r ^ 7], 192, T.LAQ, T.LAS, CH * (r % 4), T.sem.arrA)
    send(hq2, dB, 256, T.LAQ, T.LAS, CH * (r % 4), T.sem.arrB)
    send(hq3, dC, 384, T.LBQ, T.LBS, CH * (r % 2), T.sem.arrC)
    send(hq4, [partner], 576, T.LBQ, T.LBS, 128, T.sem.arrD)

    def finish(lo, hi, c0, banks, bufq, bufs, c):
        hp = [one(te.matmul_mx(buf[:, at:at + 128], T.WQ[:, 128 * o:128 * o + 128], T.WS[:, 128 * o:128 * o + 128],
                               bufq[:, c:c + 128], bufs[:, c:c + 128], True, True)) for o, (buf, at) in enumerate(banks)]
        hs = []
        for o, (buf, at) in enumerate(banks):
            need("sv"[o], hp[o])
            dst, inp = T.Y[:, lo:hi, o, :], buf[:, at + c0:at + c0 + CH * (hi - lo)]
            hs.append(one(v.tensor_copy(dst, inp) if o else s.activation(dst, inp, Copy)))
        need("y", *hs)
        one(sy.dma_start(T.y[:, 128 * lo:128 * hi], T.Y[:, lo:hi]), 16)
        return hs

    g.wait_ge(T.sem.arrX, 8)
    need("g", hfill)
    for a, b in others:
        one(g.dma_start(T.ix[a:b, :], T.IXL[a:b, CH * (r % 2):CH * (r % 2) + CH, 0], accum_op=add), 16)
    need("y", hif)
    one(sy.dma_start(T.ix[r:r + 1, :], T.IF[16 * (r % 2):16 * (r % 2) + 16, :]), 16)

    need("t", hwq, hwin)
    te.wait_ge(T.sem.arrA, 32)
    hfa = finish(dA[0], dA[0] + 2, 0, ((T.SC, 0), (T.SC, 512)), T.LAQ, T.LAS, CH * (dA[0] % 4))
    te.wait_ge(T.sem.arrB, 16)
    finish(dB[0], dB[0] + 2, 0, ((T.VB0, 0), (T.SB0, 0)), T.LAQ, T.LAS, CH * (dB[0] % 4))
    need("t", hq5)
    finish(r, r + 1, CH, ((T.VB1, 0), (T.SB1, 0)), T.GQ, T.GS, 640)
    te.wait_ge(T.sem.arrC, 16)
    finish(dC[0], dC[0] + 2, 0, ((T.SC, 1024), (T.SC, 1536)), T.LBQ, T.LBS, 0)
    need("t", *hfa)
    te.wait_ge(T.sem.arrD, 16)
    finish(partner, partner + 1, CH, ((T.SC, 0), (T.SC, 512)), T.LBQ, T.LBS, 64)

    g.wait_ge(T.sem.sent, nsent[0])
    for h in events:
        if h[0] not in done and h[1]:
            need("g", h)
